import numpy as np, ml_dtypes
CORES = [13,21,141,149]
N = 4
BF = ml_dtypes.bfloat16
def gentries(a):
    return np.ascontiguousarray(a.reshape(8, 16, -1).transpose(0, 2, 1)).reshape(8, -1)
def gtable(e):
    e = np.asarray(e); return np.ascontiguousarray(e.reshape(8, -1, 16).transpose(0, 2, 1)).reshape(128, -1).astype(np.int32)
M, D, L, Q = 4096, 5, 3, 1024
S = [0, 4096, 6144, 7168, 7680, 7936, 8064]
NODES = S[-1]; FULL = 2 ** L - 1; QP = Q // N
def gtables(a):
    return np.stack([gtable(e) for e in a])
def letters(rng, *shape):
    return np.left_shift(np.uint8(1), rng.integers(0, L, shape, dtype=np.uint8))
def anyset(rng, *shape):
    return rng.integers(1, FULL + 1, shape, dtype=np.uint8)
def tobf(v):
    return v.astype(np.float32).astype(BF)
def pairs(rng):
    le = np.zeros((N, 8, NODES - M), np.int64); ri = le.copy()
    for d in range(1, D + 1):
        e = S[d - 1] + np.argsort(rng.random((N, 8, S[d] - S[d - 1])), axis=2); a, b = S[d] - M, S[d + 1] - M
        le[:, :, a:b] = e[:, :, 0::2]; ri[:, :, a:b] = e[:, :, 1::2]
    return le, ri
def nodes(rng):
    d = rng.integers(0, D + 1, (N, 8, Q)); lo = np.array(S)[d]; n = np.array(S)[d + 1] - lo
    return lo + np.minimum((rng.random((N, 8, Q)) * n).astype(np.int64), n - 1)
def setup_inputs(rng):
    le, ri = pairs(rng)
    leaf = np.where(rng.random((N, 128, M), dtype=np.float32) < 0.125, anyset(rng, N, 128, M), letters(rng, N, 128, M))
    return {"leaf": tobf(leaf), "left": gtables(le), "right": gtables(ri), "clade": gtables(nodes(rng)), "edge": gtables(nodes(rng))}
def setup_inputs_near(rng):
    d = setup_inputs(rng); rate = np.repeat(0.1 * (1 + np.arange(8)), 16).reshape(1, 128, 1).astype(np.float32)
    leaf = np.where(rng.random((N, 128, M), dtype=np.float32) < rate, d["leaf"].astype(np.float32), letters(rng, 1, 128, 1).astype(np.float32))
    d["leaf"] = tobf(leaf); return d
def setup_inputs_order(rng):
    d = setup_inputs(rng); le = np.zeros((N, 8, NODES - M), np.int64); ri = le.copy()
    for k in range(1, D + 1):
        e = np.arange(S[k - 1], S[k]); a, b = S[k] - M, S[k + 1] - M
        le[0::2, :, a:b] = e[0::2]; ri[0::2, :, a:b] = e[1::2]
        le[1::2, :, a:b] = e[::-1][0::2]; ri[1::2, :, a:b] = e[::-1][1::2]
    d["left"] = gtables(le); d["right"] = gtables(ri)
    j = np.broadcast_to(np.arange(Q), (N, 8, Q))
    d["edge"] = gtables(j); d["clade"] = gtables(NODES - 1 - j); return d
def setup_inputs_few(rng):
    d = setup_inputs(rng); p = np.array([0, M - 1, M, S[D], NODES - 1])
    d["clade"] = gtables(p[rng.integers(0, 5, (N, 8, Q))]); d["edge"] = gtables(p[rng.integers(0, 5, (N, 8, Q))]); return d
def setup_inputs_far(rng):
    d = setup_inputs_order(rng); h = M // 2
    a = rng.integers(0, L, (1, 128, 1)); b = (a + rng.integers(1, L, (1, 128, 1))) % L
    leaf = np.where(np.arange(M) < h, np.left_shift(1, a), np.left_shift(1, b))
    d["leaf"] = tobf(np.repeat(leaf, N, axis=0))
    c = rng.integers(h, M, (N, 8, Q)); mv = (rng.random((N, 8, Q)) < 0.125) & (np.arange(8).reshape(1, 8, 1) >= 4)
    d["clade"] = gtables(np.where(mv, c - h, c)); d["edge"] = gtables(rng.integers(0, h, (N, 8, Q))); return d
def setup_inputs_spread(rng):
    d = setup_inputs(rng); p = rng.random((N, 128, L)) ** 3 + 1e-6; c = np.add.accumulate(p, axis=2); c = (c / c[:, :, -1:]).astype(np.float32)
    x = rng.random((N, 128, M), dtype=np.float32); lt = np.zeros((N, 128, M), np.uint8)
    for k in range(L - 1): lt += x > c[:, :, k:k + 1]
    am = rng.choice(np.array([0, 0, 0, 0.02, 0.02, 1], np.float32), (N, 1, M))
    amb = np.where(rng.random((N, 128, M), dtype=np.float32) < 0.5, np.uint8(FULL), anyset(rng, N, 128, M))
    d["leaf"] = tobf(np.where(rng.random((N, 128, M), dtype=np.float32) < am, amb, np.left_shift(np.uint8(1), lt)))
    e = np.minimum((NODES * rng.random((N, 8, Q)) ** 4).astype(np.int64), NODES - 1); h = np.minimum((NODES * rng.random((N, 8, Q)) ** 4).astype(np.int64), NODES - 1)
    d["edge"] = gtables(e); d["clade"] = gtables(NODES - 1 - h); return d
def check_inputs(d):
    bad = []
    try:
        v = d["leaf"].astype(np.float32)
        if not ((v == np.floor(v)) & (v >= 1) & (v <= FULL)).all(): bad.append("leaf")
        ok = True
        for q in range(N):
            le, ri = gentries(d["left"][q]), gentries(d["right"][q])
            for k in range(1, D + 1):
                a, b = S[k] - M, S[k + 1] - M
                e = np.sort(np.concatenate([le[:, a:b], ri[:, a:b]], axis=1), axis=1)
                ok = ok and bool((e == np.arange(S[k - 1], S[k])).all())
        if not ok: bad.append("left and right")
        for a in ("clade", "edge"):
            if not ((d[a] >= 0) & (d[a] < NODES)).all(): bad.append(a)
    except Exception:
        bad.append("shapes")
    return bad
def fitch(a, b):
    i = a & b
    return np.where(i > 0, i, a | b)
def reference(leaf, left, right, clade, edge):
    inside = np.zeros((N, 8, 16, NODES), np.uint8); outside = np.full((N, 8, 16, NODES), FULL, np.uint8)
    inside[:, :, :, :M] = leaf.astype(np.float32).astype(np.uint8).reshape(N, 8, 16, M)
    for q in range(N):
        le, ri = gentries(left[q]), gentries(right[q])
        for g in range(8):
            u, o = inside[q, g], outside[q, g]
            for d in range(1, D + 1):
                x, z = le[g, S[d] - M:S[d + 1] - M], ri[g, S[d] - M:S[d + 1] - M]
                u[:, S[d]:S[d + 1]] = fitch(u[:, x], u[:, z])
            for d in range(D, 0, -1):
                x, z = le[g, S[d] - M:S[d + 1] - M], ri[g, S[d] - M:S[d + 1] - M]
                o[:, x] = fitch(o[:, S[d]:S[d + 1]], u[:, z])
                o[:, z] = fitch(o[:, S[d]:S[d + 1]], u[:, x])
    on = fitch(inside, outside); c = np.zeros((N, 8, Q), np.int64)
    for r in range(N):
        cl, ed = gentries(clade[r]), gentries(edge[r])
        for g in range(8):
            for q in range(N):
                j = slice(q * QP, (q + 1) * QP)
                c[r, g, j] = np.sum((inside[q, g][:, cl[g, j]] & on[r, g][:, ed[g, j]]) == 0, axis=0)
    runs = c.reshape(N, 8, 8, Q // 8)
    return {"cost": np.min(runs, axis=2).astype(np.float32), "first": np.argmin(runs, axis=2).astype(np.float32)}

@@ -1,0 +1,554 @@
+from concourse.bass import DstId, RemoteDMATransfer
+from concourse.mybir import AluOpType, ActivationFunctionType
+
+S = [0, 4096, 6144, 7168, 7680, 7936, 8064]
+ONES = 1 + 64 + 4096 + 262144
+M21 = 21 * ONES
+PB = 64
+
+SCRATCH = {
+    "lf": ("sbuf", [128, 4096], "bfloat16"),
+    "x": ("sbuf", [128, 8064], "bfloat16"),
+    "li": ("sbuf", [128, 248], "int32"),
+    "ri": ("sbuf", [128, 248], "int32"),
+    "cl": ("sbuf", [128, 64], "int32"),
+    "ed": ("sbuf", [128, 64], "int32"),
+    "req": ("sbuf", [128, 64], "int32"),
+    "off": ("sbuf", [128, 496], "uint16"),
+    "qo": ("sbuf", [128, 528], "uint16"),
+    "qi": ("sbuf", [128, 384], "int32"),
+    "c1": ("sbuf", [128, 4112], "bfloat16"),
+    "c2": ("sbuf", [128, 2064], "bfloat16"),
+    "c3": ("sbuf", [128, 1792], "bfloat16"),
+    "u": ("sbuf", [128, 3968], "int32"),
+    "o": ("sbuf", [128, 1920], "bfloat16"),
+    "pay": ("sbuf", [128, 4096], "float32"),
+    "sl0": ("sbuf", [128, 4104], "float32"),
+    "sl1": ("sbuf", [128, 2056], "float32"),
+    "gs": ("sbuf", [128, 1024], "float32"),
+    "gq": ("sbuf", [128, 5120], "bfloat16"),
+    "dn": ("sbuf", [128, 1024], "int32"),
+    "ta": ("sbuf", [128, 768], "int32"),
+    "tb": ("sbuf", [128, 768], "int32"),
+    "pre": ("sbuf", [128, 768], "int32"),
+    "snd": ("sbuf", [128, 192], "int32"),
+    "land": ("sbuf", [128, 256], "int32"),
+    "nzf": ("sbuf", [128, 256], "float32"),
+    "xi": ("sbuf", [128, 128], "float32"),
+    "yi": ("sbuf", [128, 16], "int32"),
+    "w": ("sbuf", [128, 1024], "bfloat16"),
+    "bm": ("sbuf", [128, 144], "float32"),
+    "gm": ("sbuf", [128, 40], "float32"),
+    "kc": ("sbuf", [128, 128], "float32"),
+    "ki": ("sbuf", [128, 160], "int32"),
+    "kf": ("sbuf", [128, 224], "float32"),
+    "kb": ("sbuf", [128, 16], "bfloat16"),
+    "ei": ("sbuf", [128, 384], "int32"),
+    "ef": ("sbuf", [128, 256], "float32"),
+}
+for _b in range(8):
+    SCRATCH["ps%d" % _b] = ("psum", [128, 512], "float32")
+
+SEMAPHORES = ["v", "a", "p", "g", "dl0", "dl1", "dl2", "dl3", "dli", "dri", "dcl", "ded", "drq", "do1", "do2",
+              "rq", "rp", "snt"]
+
+NE = 4
+
+
+def first_hops(src, T, topo):
+    free = [c for c in topo.cores_of(src) if T.rank_of(c) is None]
+    free.sort(key=lambda c: topo.die(c) != topo.die(src))
+    hops = {}
+    for d in T.cores:
+        if d == src:
+            continue
+        if topo.may_write(src, d):
+            hops[d] = d
+        else:
+            r = [c for c in free if topo.may_write(c, d)][0]
+            free.remove(r)
+            hops[d] = r
+    return hops
+
+
+def bits(engs):
+    return sum(1 << e for e in engs)
+
+
+def relay_program(g, core, T, topo, src, dst):
+    n = len(T.cores)
+    r, q = T.rank_of(src), T.rank_of(dst)
+    rid, pid = topo.addr(dst, core)
+    m = bits(topo.engines(core, dst)[:NE])
+    sl = (r - q - 1) % n
+    g.wait_ge(T.sem.rq, NE)
+    g.remote_dma(T.req[:, 16 * sl:16 * sl + 16], T.req[:, 0:16], T.sem.rq, T.sem.snt, pid, rid, m)
+    g.wait_ge(T.sem.rp, NE)
+    g.remote_dma(T.land[:, 64 * r:64 * r + 64], T.land[:, 0:64], T.sem.rp, T.sem.snt, pid, rid, m)
+    g.wait_ge(T.sem.snt, 2 * NE)
+
+
+def rank_program(g, core, T, topo):
+    me = T.rank_of(core)
+    if me is None:
+        for src in T.cores:
+            for d, h in first_hops(src, T, topo).items():
+                if h == core:
+                    relay_program(g, core, T, topo, src, d)
+        return
+    n = len(T.cores)
+    A, F = AluOpType, ActivationFunctionType
+    Q = {"v": g.vector, "a": g.scalar, "p": g.tensor, "g": g, "s": g.sync}
+    cnt = {"v": 0, "a": 0, "p": 0, "g": 0}
+    waited = {e: {} for e in Q}
+    wr, rd = {}, {}
+
+    def wait(e, tok):
+        if waited[e].get(tok[0], 0) < tok[1]:
+            Q[e].wait_ge(T.sem[tok[0]], tok[1])
+            waited[e][tok[0]] = tok[1]
+
+    def ap(r):
+        return T[r[0]][:, r[1]:r[2]]
+
+    def span(r):
+        return (r[0], 0, 512) if r[0].startswith("ps") else r
+
+    def order(e, reads, writes):
+        need = {}
+        for r, logs in [(x, (wr,)) for x in reads] + [(x, (wr, rd)) for x in writes]:
+            nm, lo, hi = span(r)
+            for log in logs:
+                for (l2, h2, tok) in log.get(nm, []):
+                    if l2 < hi and lo < h2 and not (e == "p" and tok[0] == "p"):
+                        need[tok[0]] = max(need.get(tok[0], 0), tok[1])
+        for k in need:
+            wait(e, (k, need[k]))
+
+    def note(tok, reads, writes):
+        for r in reads:
+            nm, lo, hi = span(r)
+            rd.setdefault(nm, []).append((lo, hi, tok))
+        for r in writes:
+            nm, lo, hi = span(r)
+            wr.setdefault(nm, []).append((lo, hi, tok))
+
+    def op(e, fn, reads, writes):
+        order(e, reads, writes)
+        ins = fn()
+        cnt[e] += 1
+        ins.then_inc(T.sem[e], 1)
+        note((e, cnt[e]), reads, writes)
+
+    def ts(out, in0, s1, op0, s2=None, op1=None):
+        if op1 is None:
+            op("v", lambda: g.vector.tensor_scalar(ap(out), ap(in0), s1, None, op0), [in0], [out])
+        else:
+            op("v", lambda: g.vector.tensor_scalar(ap(out), ap(in0), s1, s2, op0, op1), [in0], [out])
+
+    def tt(out, a, b, o):
+        op("v", lambda: g.vector.tensor_tensor(ap(out), ap(a), ap(b), o), [a, b], [out])
+
+    def cp(out, a):
+        op("v", lambda: g.vector.tensor_copy(ap(out), ap(a)), [a], [out])
+
+    def fill(out, c):
+        op("v", lambda: g.vector.memset(ap(out), c), [], [out])
+
+    def gather(e, out, win, off):
+        if e == "v":
+            op("v", lambda: g.vector.tensor_copy(ap(out), ap(win).indirect(ap(off))), [win, off], [out])
+        else:
+            op("a", lambda: g.scalar.activation(ap(out), ap(win).indirect(ap(off)), F.Copy), [win, off], [out])
+
+    def scatter(e, win, off, src):
+        if e == "v":
+            op("v", lambda: g.vector.tensor_copy(ap(win).indirect(ap(off)), ap(src)), [src, off], [win])
+        else:
+            op("a", lambda: g.scalar.activation(ap(win).indirect(ap(off)), ap(src), F.Silu), [src, off], [win])
+
+    def mm(out_ap, out, terms):
+        reads = [r for t in terms for r in t[2]]
+
+        def fn():
+            for i, t in enumerate(terms):
+                ins = g.tensor.matmul(out_ap, t[0], t[1], i == 0, i == len(terms) - 1)
+            return ins
+        op("p", fn, reads, [out])
+
+    def pack(out, fields, nine=False):
+        terms = []
+        for s, rs in enumerate(fields):
+            wt = ("w", 128 * (s + 4 * nine), 128 * (s + 4 * nine) + 128)
+            for r in rs:
+                terms.append((ap(wt), ap(r), [wt, r]))
+        mm(ap(out), out, terms)
+
+    def sub(r, a, b):
+        return (r[0], r[1] + a, r[1] + b)
+
+    def pack_cand(out, srcs, nine=False, blocks=range(4)):
+        for j, q in enumerate(blocks):
+            pack(sub(out, 64 * j, 64 * j + 64),
+                 [[sub(r, 256 * q + 64 * s, 256 * q + 64 * s + 64) for r in srcs] for s in range(4)], nine)
+
+    def empty_bits(si, b):
+        ts(b, si, 1, A.logical_shift_right, M21, A.bitwise_and)
+        yield
+        ts(b, b, -1.0, A.mult, float(32 * ONES), A.add)
+        yield
+        ts(b, b, 5, A.logical_shift_right, ONES, A.bitwise_and)
+        yield
+
+    def fitch(src, a, b):
+        if src != a:
+            cp(a, src)
+            yield
+        yield from empty_bits(a, b)
+        ts(b, b, 21.0, A.mult)
+        yield
+        tt(b, b, src, A.add)
+        yield
+
+    def unpack(b, outs):
+        for s, r in enumerate(outs):
+            ts(r, b, 6 * s + 1, A.logical_shift_right, 21, A.bitwise_and)
+            yield
+
+    def late(k, gen):
+        for _ in range(k):
+            yield
+        yield from gen
+
+    def run(*gens):
+        gens = list(gens)
+        while gens:
+            for x in list(gens):
+                if next(x, "end") == "end":
+                    gens.remove(x)
+
+    def load(e, sem, out, src):
+        Q[e].dma_start(ap(out), src).then_inc(T.sem[sem], 16)
+        note((sem, 16), [], [out])
+
+    def U(a, b):
+        return ("u", a - 4096, b - 4096)
+
+    def X(a, b):
+        return ("x", a, b)
+
+    def O(a, b):
+        return ("o", a - 6144, b - 6144)
+
+    def OFF(d, side, a, b):
+        c = (2 * (S[d] - 4096) + side * (S[d + 1] - S[d])) // 16
+        return ("off", c + a // 16, c + b // 16)
+
+    def C(d, side, a, b):
+        nd = S[d + 1] - S[d]
+        nm, base = {1: ("c1", 0), 2: ("c2", 0), 3: ("c3", 0), 4: ("c3", 1024), 5: ("c3", 1536)}[d]
+        return (nm, base + side * nd + a, base + side * nd + b)
+
+    def QO(i):
+        return ("qo", 64 * i, 64 * i + 64)
+
+    def QI(i):
+        return ("qi", 64 * i, 64 * i + 64)
+
+    def GQ(i):
+        return ("gq", 1024 * i, 1024 * i + 1024)
+
+    def PS(b, a, c):
+        return ("ps%d" % b, a, c)
+
+    load("a", "dri", ("ri", 0, 248), T.right[:])
+    load("s", "dli", ("li", 0, 248), T.left[:])
+    NL = 4
+    LW = 4096 // NL
+    for j in range(NL):
+        load("s", "dl%d" % j, ("lf", LW * j, LW * j + LW), T.leaf[:, LW * j:LW * j + LW])
+    load("s", "dcl", ("cl", 0, 64), T.clade[:])
+    load("s", "ded", ("ed", 0, 64), T.edge[:])
+    load("s", "drq", ("req", 48, 64), T.clade[:, 16 * me:16 * me + 16])
+
+    def iota(out, pat, base, cm, fl=True):
+        if fl:
+            op("g", lambda: g.iota(ap(out), pat, base, cm, allow_small_or_imprecise_dtypes=True), [], [out])
+        else:
+            op("g", lambda: g.iota(ap(out), pat, base, cm), [], [out])
+
+    def narrow(a, b):
+        op("g", lambda: g.affine_select(ap(X(a, b)), ap(U(a, b)), [[0, b - a]], A.is_gt, 0.0, 1, 0), [U(a, b)], [X(a, b)])
+
+    iota(("xi", 0, 128), [[1, 128]], 0, -1)
+    iota(("yi", 0, 8), [[-16, 8]], 0, 1, False)
+    iota(("pay", 0, 1024), [[1, 1024]], PB, 0)
+
+    fill(("c1", 4096, 4112), 7.0)
+    fill(("c2", 2048, 2064), 21.0)
+    fill(O(S[5], S[6]), 21.0)
+    fill(("sl0", 4096, 4104), float(4096 + PB))
+    fill(("sl1", 2048, 2056), float(2048 + PB))
+    fill(("bm", 0, 144), 0.0)
+    fill(("gm", 0, 40), 0.0)
+    for s in range(8):
+        ts(("w", 128 * s, 128 * s + 128), ("xi", 0, 128), 0.0, A.is_equal, float(64 ** (s % 4) * (9 if s >= 4 else 1)), A.mult)
+    ts(("yi", 8, 16), ("yi", 0, 8), 4, A.arith_shift_right)
+    op("v", lambda: g.vector.tensor_scalar(T.bm[:, 16:144:16], T.yi[:, 0:8], 0.0, None, A.is_equal),
+       [("yi", 0, 8)], [("bm", 0, 144)])
+    op("v", lambda: g.vector.tensor_scalar(T.gm[:, 3:35:4], T.yi[:, 8:16], 0.0, None, A.is_equal),
+       [("yi", 8, 16)], [("gm", 0, 40)])
+
+    for d in range(1, 6):
+        for side in (1, 0):
+            nd = S[d + 1] - S[d]
+            ts(OFF(d, side, 0, nd), ("ri" if side else "li", (S[d] - 4096) // 16, (S[d + 1] - 4096) // 16),
+               float(S[d - 1]), A.subtract)
+    ts(("qo", 512, 520), ("ri", 240, 248), float(S[4]), A.subtract)
+    ts(("qo", 520, 528), ("li", 240, 248), float(S[4]), A.subtract)
+
+    hops = first_hops(core, T, topo)
+    dests = sorted(hops, key=lambda d: len(topo.engines(core, hops[d])))
+    used, masks = [], {}
+    for d in dests:
+        es = topo.engines(core, hops[d])
+        es = [e for e in (es if hops[d] == d else es[::-1]) if e not in used][:NE]
+        used += es
+        masks[d] = bits(es)
+
+    def send(src_of, dst_of, sem, reads):
+        order("g", reads, [])
+        trs = []
+        for d in dests:
+            rid, pid = topo.addr(hops[d], core)
+            trs.append(RemoteDMATransfer(dst_ids=[DstId(rid=rid, pnc=pid)], dma_engine_mask=masks[d], remote_sem=sem,
+                                         src=src_of(T.rank_of(d)), dst=dst_of(T.rank_of(d), hops[d] == d)))
+        g.remote_dma_fused(trs, local_sem=T.sem.snt)
+
+    iota(("pay", 1024, 2048), [[1, 1024]], PB + 1024, 0)
+    send(lambda q: T.cl[:, 16 * q:16 * q + 16],
+         lambda q, direct: T.req[:, 16 * ((me - q - 1) % n) * direct:16 * ((me - q - 1) % n) * direct + 16],
+         T.sem.rq, [("cl", 0, 64)])
+    note(("rq", NE * (n - 1)), [], [("req", 0, 48)])
+    iota(("pay", 2048, 3072), [[1, 1024]], PB + 2048, 0)
+    iota(("pay", 3072, 4096), [[1, 1024]], PB + 3072, 0)
+
+    SL0, SL1 = ("sl0", 0, 4096), ("sl1", 0, 2048)
+    at0, at1 = [0], [0]
+
+    def slots(e, d, m):
+        at, half = ((at0, 2048), (at1, 1024))[d]
+        while m > 0 and at[0] < 2 * half:
+            a = at[0]
+            b = min(a + m, (a // half + 1) * half)
+            scatter(e, (SL0, SL1)[d], OFF(d + 1, 1 - a // half, a % half, a % half + b - a), ("pay", a, b))
+            m -= b - a
+            at[0] = b
+
+    slots("a", 0, 512)
+    slots("v", 1, 512)
+    for j in range(NL - 1):
+        ts(X(LW * j, LW * j + LW), ("lf", LW * j, LW * j + LW), 9.0, A.mult)
+
+    LF = ("lf", 0, 4096)
+    CH = (256, 256, 512, 512, 256, 256)
+    lo = 0
+    for j, m in enumerate(CH):
+        for side in (0, 1):
+            gather("v" if j == 0 else "a", C(1, side, lo, lo + m), LF, OFF(1, side, lo, lo + m))
+        lo += m
+
+    def level1(j, lo, hi):
+        wd = (hi - lo) // 4
+        for side in (0, 1):
+            pack(PS(j, wd * side, wd * side + wd),
+                 [[C(1, side, lo + wd * s, lo + wd * s + wd)] for s in range(4)], True)
+        t = ("dn", lo // 2, hi // 2)
+        a, b = ("ta", lo // 4, hi // 4), ("tb", lo // 4, hi // 4)
+        cp(t, PS(j, 0, 2 * wd))
+        yield
+        ts(t, t, M21, A.bitwise_and)
+        yield
+        tt(a, sub(t, 0, wd), sub(t, wd, 2 * wd), A.add)
+        yield
+        yield from fitch(a, a, b)
+        yield from unpack(b, [U(4096 + lo + wd * s, 4096 + lo + wd * s + wd) for s in range(4)])
+
+    lo = 0
+    for j in range(0, len(CH), 2):
+        m, m2 = CH[j], CH[j + 1]
+        run(level1(j % 4, lo, lo + m), level1((j + 1) % 4, lo + m, lo + m + m2))
+        if j == 0:
+            ts(X(4096 - LW, 4096), ("lf", 4096 - LW, 4096), 9.0, A.mult)
+            ed = ("ed", 0, 64)
+            ts(QO(0), ed, 4096.0, A.min)
+            cp(QO(1), ed)
+            ts(QI(0), ed, 4096.0, A.subtract)
+            ts(QI(1), ed, 6144.0, A.subtract)
+        narrow(4096 + lo, 4096 + lo + m + m2)
+        lo += m + m2
+    slots("a", 0, 1536)
+
+    def kids(e, d, lo, hi):
+        win = U(S[d - 1], S[d]) if e == "v" else X(S[d - 1], S[d])
+        if hi - lo == S[d + 1] - S[d]:
+            gather(e, sub(C(d, 0, 0, 0), 0, 2 * hi), win, sub(OFF(d, 0, 0, 0), 0, hi // 8))
+        else:
+            for side in (0, 1):
+                gather(e, C(d, side, lo, hi), win, OFF(d, side, lo, hi))
+
+    def up_pack(d, lo, hi, k, bank):
+        wd = (hi - lo) // k
+        pack(PS(bank, 0, wd), [[C(d, side, lo + wd * s, lo + wd * s + wd) for side in (0, 1)] for s in range(k)])
+
+    def up(d, lo, hi, k, bank, t0):
+        wd = (hi - lo) // k
+        a, b = ("ta", t0, t0 + wd), ("tb", t0, t0 + wd)
+        yield from fitch(PS(bank, 0, wd), a, b)
+        yield from unpack(b, [U(S[d] + lo + wd * s, S[d] + lo + wd * s + wd) for s in range(k)])
+
+    GS = ("gs", 0, 1024)
+
+    def to_list(bank):
+        mm(T["ps%d" % bank][:, 0:64], PS(bank, 0, 64),
+           [(T.bm[:, 16 - s:144 - s], T.gs[:, s:1024:16], [("bm", 0, 144), GS]) for s in range(16)])
+
+    for i in range(4):
+        kids("v" if i < 2 else "a", 2, 256 * i, 256 * i + 256)
+        up_pack(2, 256 * i, 256 * i + 256, 4, 4 + i)
+    for i in (0, 2):
+        run(up(2, 256 * i, 256 * i + 256, 4, 4 + i, 512 + 64 * i), up(2, 256 * i + 256, 256 * i + 512, 4, 5 + i, 576 + 64 * i))
+        narrow(S[2] + 256 * i, S[2] + 256 * i + 512)
+    for i in range(2):
+        kids("v", 3, 256 * i, 256 * i + 256)
+        up_pack(3, 256 * i, 256 * i + 256, 4, i)
+    slots("a", 0, 4096)
+    gather("a", GS, ("sl0", 0, 4104), QO(0))
+    cp(QO(2), ("req", 0, 64))
+    run(up(3, 0, 256, 4, 0, 0), late(3, up(3, 256, 512, 4, 1, 64)))
+    narrow(S[3], S[4])
+    kids("v", 4, 0, 256)
+    up_pack(4, 0, 256, 4, 2)
+    slots("v", 1, 128)
+    run(up(4, 0, 256, 4, 2, 128))
+    narrow(S[4], S[5])
+    kids("v", 5, 0, 128)
+    up_pack(5, 0, 128, 2, 4)
+
+    scatter("v", O(S[4], S[5]), ("qo", 512, 528), ("c3", 1536, 1792))
+
+    def down_pack(d, lo, hi, bank):
+        h = (hi - lo) // 2
+        pack(PS(bank, 0, h), [[O(S[d + 1] + lo + h * (s % 2), S[d + 1] + lo + h * (s % 2) + h),
+                               C(d + 1, 1 - s // 2, lo + h * (s % 2), lo + h * (s % 2) + h)] for s in range(4)])
+
+    def down(d, lo, hi, bank, t0):
+        h, npar = (hi - lo) // 2, S[d + 2] - S[d + 1]
+        a, b = ("ta", t0, t0 + h), ("tb", t0, t0 + h)
+        yield from fitch(PS(bank, 0, h), a, b)
+        c0 = [npar * (s // 2) + lo + h * (s % 2) for s in range(4)]
+        yield from unpack(b, [("dn", c, c + h) for c in c0])
+
+    def down_scatter(d):
+        npar = S[d + 2] - S[d + 1]
+        scatter("v", O(S[d], S[d + 1]), sub(OFF(d + 1, 0, 0, 0), 0, npar // 8), ("dn", 0, 2 * npar))
+
+    def step(bank, i_s, i_t, mask, prev, o_sib, o_next, cap):
+        ts(QI(i_s), PS(bank, 0, 64), float(PB), A.subtract)
+        ts(QI(i_t), QI(i_s), mask, A.bitwise_and)
+        cp(QO(o_sib), QI(i_s))
+        tt(QI(i_t), QI(i_t), prev, A.max)
+        ts(QO(o_next), QI(i_t), float(cap), A.min)
+
+    XA = X(0, S[6])
+    down_pack(3, 0, 256, 1)
+    to_list(6)
+    run(up(5, 0, 128, 2, 4, 192), late(3, down(3, 0, 256, 1, 256)))
+    narrow(S[5], S[6])
+    iota(("kc", 0, 128), [[1, 2], [0, 16], [2, 4]], 0, 0)
+    slots("a", 1, 2048)
+    down_scatter(3)
+    down_pack(2, 0, 256, 2)
+    down_pack(2, 256, 512, 4)
+    step(6, 2, 3, 2047, QI(0), 4, 5, 2048)
+    gather("a", GQ(1), XA, QO(2))
+    pack_cand(PS(0, 0, 256), [GQ(1)])
+    gather("a", GS, ("sl1", 0, 2056), QO(5))
+    to_list(7)
+    gather("a", GQ(2), ("c1", 0, 4112), QO(4))
+    pack_cand(PS(1, 0, 256), [GQ(2)], True)
+    gather("a", GQ(0), XA, QO(1))
+    pack_cand(PS(1, 256, 512), [GQ(0)])
+    run(down(2, 0, 256, 2, 384), late(3, down(2, 256, 512, 4, 512)))
+    down_scatter(2)
+    step(7, 4, 5, 1023, QI(1), 6, 7, 1919)
+    for h in range(4):
+        gather("a", sub(GQ(3), 256 * h, 256 * h + 256), ("c2", 0, 2064), sub(QO(6), 16 * h, 16 * h + 16))
+        gather("a", sub(GQ(4), 256 * h, 256 * h + 256), ("o", 0, 1920), sub(QO(7), 16 * h, 16 * h + 16))
+
+    CLM, PR = ("pre", 512, 768), ("pre", 0, 512)
+    cp(CLM, PS(0, 0, 256))
+    ts(("kc", 0, 128), ("kc", 0, 128), 0.125, A.mult)
+    ts(("snd", 0, 192), sub(CLM, 0, 192), M21, A.bitwise_and)
+    ts(("land", 64 * me, 64 * me + 64), sub(CLM, 192, 256), M21, A.bitwise_and)
+    send(lambda q: T.snd[:, 64 * ((q - me - 1) % n):64 * ((q - me - 1) % n) + 64],
+         lambda q, direct: T.land[:, 64 * me * direct:64 * me * direct + 64],
+         T.sem.rp, [("snd", 0, 192)])
+    note(("rp", NE * (n - 1)), [], [("land", 64 * q, 64 * q + 64) for q in range(n) if q != me])
+    cp(PR, PS(1, 0, 512))
+    ts(PR, PR, M21, A.bitwise_and)
+
+    def chain(q0, q1, bank):
+        lo, hi = 64 * q0, 64 * q1
+        wd = hi - lo
+        pack_cand(PS(bank, 0, wd), [GQ(4), GQ(3)], blocks=range(q0, q1))
+        a, b = ("ta", lo, hi), ("tb", lo, hi)
+        yield from fitch(PS(bank, 0, wd), a, b)
+        for i, nxt in enumerate((("pre", lo, hi), ("pre", 256 + lo, 256 + hi), ("land", lo, hi))):
+            ts(b, b, 1, A.logical_shift_right, M21, A.bitwise_and)
+            yield
+            tt(a, b, nxt, A.add)
+            yield
+            if i < 2:
+                yield from fitch(a, a, b)
+        yield from empty_bits(a, b)
+        cp(("nzf", lo, hi), b)
+        for q in range(q0, q1):
+            op("p", lambda: g.tensor.matmul(T.ps7[0:64, 0:32], T.nzf[:, 64 * q:64 * q + 64], T.gm[:, 3 - q:35 - q], q == 0, q == 3),
+               [("nzf", 64 * q, 64 * q + 64), ("gm", 0, 40)], [PS(7, 0, 32)])
+        yield
+
+    run(chain(0, 2, 2), late(2, chain(2, 4, 4)))
+
+    V = g.vector
+    op("v", lambda: V.tensor_copy(T.ki[0:64, 0:32], T.ps7[0:64, 0:32]), [PS(7, 0, 32)], [("ki", 0, 32)])
+    for s in range(4):
+        op("v", lambda: V.tensor_scalar(T.ki[0:64, 32 + 32 * s:64 + 32 * s], T.ki[0:64, 0:32], 6 * s, 63,
+                                        A.logical_shift_right, A.bitwise_and), [("ki", 0, 32)], [("ki", 32 + 32 * s, 64 + 32 * s)])
+    op("v", lambda: V.tensor_tensor(T.kf[0:64, 0:128], T.ki[0:64, 32:160], T.kc[0:64, :], A.add),
+       [("ki", 32, 160), ("kc", 0, 128)], [("kf", 0, 128)])
+    op("v", lambda: V.tensor_tensor(T.kf[0:64, 128:192], T.kf[0:64, 0:64], T.kf[0:64, 64:128], A.min),
+       [("kf", 0, 128)], [("kf", 128, 192)])
+    op("v", lambda: V.tensor_tensor(T.kf[0:64, 192:224], T.kf[0:64, 128:192:2], T.kf[0:64, 129:192:2], A.min),
+       [("kf", 128, 192)], [("kf", 192, 224)])
+    op("v", lambda: V.tensor_tensor(T.kb[0:64, 0:16], T.kf[0:64, 192:224:2], T.kf[0:64, 193:224:2], A.min),
+       [("kf", 192, 224)], [("kb", 0, 16)])
+    for h in range(2):
+        mm(T.ps3[0:8, 64 * h:64 * h + 64], PS(3, 0, 128),
+           [(T.kb[0:64, 8 * h:8 * h + 8], T.w[0:64, 0:64], [("kb", 0, 16), ("w", 0, 128)])])
+    op("v", lambda: V.tensor_scalar(T.ei[0:8, 0:128], T.ps3[0:8, 0:128], 8.0, None, A.mult), [PS(3, 0, 128)], [("ei", 0, 128)])
+    op("v", lambda: V.tensor_scalar(T.ei[0:8, 128:256], T.ei[0:8, 0:128], 3, None, A.logical_shift_right),
+       [("ei", 0, 128)], [("ei", 128, 256)])
+    op("v", lambda: V.tensor_scalar(T.ei[0:8, 256:384], T.ei[0:8, 0:128], 7, None, A.bitwise_and),
+       [("ei", 0, 128)], [("ei", 256, 384)])
+    op("v", lambda: V.tensor_copy(T.ef[0:8, 0:256], T.ei[0:8, 128:384]), [("ei", 128, 384)], [("ef", 0, 256)])
+    order("s", [("ef", 0, 256)], [])
+    g.sync.dma_start(T.cost[:], T.ef[0:8, 0:128]).then_inc(T.sem.do1, 16)
+    order("a", [("ef", 0, 256)], [])
+    g.scalar.dma_start(T.first[:], T.ef[0:8, 128:256]).then_inc(T.sem.do2, 16)
+
+    for e in cnt:
+        wait("g", (e, cnt[e]))
+    wait("g", ("snt", 2 * NE * (n - 1)))
+    wait("g", ("do1", 16))
+    wait("g", ("do2", 16))

@@ -1,58 +1,79 @@
 from concourse.bass import DstId, RemoteDMATransfer
-from concourse.mybir import AluOpType, ActivationFunctionType
+from concourse.mybir import AluOpType, ActivationFunctionType, AxisListType
 
 S = [0, 4096, 6144, 7168, 7680, 7936, 8064]
 ONES = 1 + 64 + 4096 + 262144
 M21 = 21 * ONES
 PB = 64
+PAD = 16
+BIG = 8192.0
+B = [2048 - (2048 >> d) for d in range(7)]
 
 SCRATCH = {
     "lf": ("sbuf", [128, 4096], "bfloat16"),
-    "x": ("sbuf", [128, 8064], "bfloat16"),
+    "c1": ("sbuf", [128, 4096], "bfloat16"),
     "li": ("sbuf", [128, 248], "int32"),
     "ri": ("sbuf", [128, 248], "int32"),
     "cl": ("sbuf", [128, 64], "int32"),
-    "ed": ("sbuf", [128, 64], "int32"),
-    "req": ("sbuf", [128, 64], "int32"),
-    "off": ("sbuf", [128, 496], "uint16"),
-    "qo": ("sbuf", [128, 528], "uint16"),
-    "qi": ("sbuf", [128, 384], "int32"),
-    "c1": ("sbuf", [128, 4112], "bfloat16"),
-    "c2": ("sbuf", [128, 2064], "bfloat16"),
-    "c3": ("sbuf", [128, 1792], "bfloat16"),
-    "u": ("sbuf", [128, 3968], "int32"),
-    "o": ("sbuf", [128, 1920], "bfloat16"),
-    "pay": ("sbuf", [128, 4096], "float32"),
-    "sl0": ("sbuf", [128, 4104], "float32"),
-    "sl1": ("sbuf", [128, 2056], "float32"),
-    "gs": ("sbuf", [128, 1024], "float32"),
-    "gq": ("sbuf", [128, 5120], "bfloat16"),
-    "dn": ("sbuf", [128, 1024], "int32"),
-    "ta": ("sbuf", [128, 768], "int32"),
-    "tb": ("sbuf", [128, 768], "int32"),
-    "pre": ("sbuf", [128, 768], "int32"),
-    "snd": ("sbuf", [128, 192], "int32"),
-    "land": ("sbuf", [128, 256], "int32"),
-    "nzf": ("sbuf", [128, 256], "float32"),
-    "xi": ("sbuf", [128, 128], "float32"),
-    "yi": ("sbuf", [128, 16], "int32"),
-    "w": ("sbuf", [128, 1024], "bfloat16"),
-    "bm": ("sbuf", [128, 144], "float32"),
-    "gm": ("sbuf", [128, 40], "float32"),
-    "kc": ("sbuf", [128, 128], "float32"),
-    "ki": ("sbuf", [128, 160], "int32"),
-    "kf": ("sbuf", [128, 224], "float32"),
+    "qv": ("sbuf", [128, 128], "int32"),
+    "lh": ("sbuf", [128, 256], "float16"),
+    "wx": ("sbuf", [128, 512], "float16"),
+    "lx": ("sbuf", [128, 256], "float16"),
+    "ws": ("sbuf", [128, 2048], "float16"),
     "kb": ("sbuf", [128, 16], "bfloat16"),
-    "ei": ("sbuf", [128, 384], "int32"),
-    "ef": ("sbuf", [128, 256], "float32"),
+    "off": ("sbuf", [128, 240], "uint16"),
+    "pi": ("sbuf", [128, 256], "uint16"),
+    "qo": ("sbuf", [128, 640], "uint16"),
+    "qi": ("sbuf", [128, 512], "int32"),
+    "big": ("sbuf", [128, 8192], "float32"),
+    "pay": ("sbuf", [128, 4096], "float32"),
+    "pos": ("sbuf", [128, 4096], "float32"),
+    "xa": ("sbuf", [128, 2048], "float32"),
+    "low": ("sbuf", [128, 320], "float32"),
+    "xh": ("sbuf", [128, 2048], "bfloat16"),
+    "xv": ("sbuf", [128, 5120], "float32"),
+    "so": ("sbuf", [128, 1024], "float32"),
+    "u": ("sbuf", [128, 2048], "int32"),
+    "uf": ("sbuf", [128, 2048], "float32"),
+    "us": ("sbuf", [128, 2048], "float32"),
+    "af": ("sbuf", [128, 2048], "float32"),
+    "ai": ("sbuf", [128, 512], "int32"),
+    "o": ("sbuf", [128, 512], "int32"),
+    "ta": ("sbuf", [128, 512], "int32"),
+    "tb": ("sbuf", [128, 512], "int32"),
+    "land": ("sbuf", [128, 448], "float32"),
+    "qp": ("sbuf", [128, 128], "int32"),
+    "pl": ("sbuf", [128, 8], "uint16"),
+    "nzf": ("sbuf", [128, 256], "float32"),
+    "sb": ("sbuf", [128, 640], "bfloat16"),
+    "m2": ("sbuf", [128, 384], "float32"),
+    "xi": ("sbuf", [128, 144], "float32"),
+    "ym": ("sbuf", [128, 256], "bfloat16"),
+    "yi": ("sbuf", [128, 72], "int32"),
+    "cf": ("sbuf", [128, 72], "float32"),
+    "wp": ("sbuf", [128, 136], "bfloat16"),
+    "we": ("sbuf", [128, 272], "float32"),
+    "wi": ("sbuf", [128, 128], "bfloat16"),
+    "wf": ("sbuf", [128, 64], "float32"),
+    "bm": ("sbuf", [128, 144], "float32"),
+    "bh": ("sbuf", [128, 144], "bfloat16"),
+    "bt": ("sbuf", [128, 144], "bfloat16"),
+    "gm": ("sbuf", [128, 32], "float32"),
+    "kc": ("sbuf", [128, 128], "float32"),
+    "ki": ("sbuf", [128, 128], "int32"),
+    "kf": ("sbuf", [128, 240], "float32"),
+    "ei": ("sbuf", [128, 128], "int32"),
+    "ef": ("sbuf", [128, 384], "float32"),
 }
 for _b in range(8):
     SCRATCH["ps%d" % _b] = ("psum", [128, 512], "float32")
 
-SEMAPHORES = ["v", "a", "p", "g", "dl0", "dl1", "dl2", "dl3", "dli", "dri", "dcl", "ded", "drq", "do1", "do2",
-              "rq", "rp", "snt"]
+SEMAPHORES = ["v", "a", "p", "g", "dl0", "dl1", "dli", "dri", "dcl", "ded", "drq", "do1", "do2",
+              "t00", "t01", "t02", "t03", "t04", "t05", "t10", "t11", "t12", "t13", "t14", "t21", "t22", "t23", "d0", "d1", "d2", "d3", "d4", "d5", "d6", "d7", "dp0", "dp1", "dc0", "dc1", "rq", "rp", "rp2", "snt"]
 
-NE = 4
+OPT = {"lv": (512, 512, 1024, 512), "lag": 3, "ne": 8, "llc": 1024, "a0": (0, 8), "junk": 6, "late": 12,
+       "le": (("a", 0), ("v", 1)), "ix": (0, 1), "ev": "avavavav",
+       "ops": (("v", 0, 0), ("v", 0, 1), ("a", 1, 0), ("a", 1, 1))}
 
 
 def first_hops(src, T, topo):
@@ -75,17 +96,44 @@ def bits(engs):
     return sum(1 << e for e in engs)
 
 
+def engine_sets(src, T, topo):
+    hops = first_hops(src, T, topo)
+    far = [d for d in hops if hops[d] == d]
+    near = [d for d in hops if hops[d] != d]
+    out = topo.engines(src, far[0])
+    rest = [e for e in topo.engines(src, hops[near[0]]) if e not in out]
+    sets = {}
+    for ds, es in ((far, out), (near, rest)):
+        k = len(es) // len(ds)
+        for i, d in enumerate(ds):
+            sets[d] = es[k * i:k * i + k][:OPT["ne"]]
+    return sets
+
+
+def peers(c, T, topo):
+    hops = first_hops(c, T, topo)
+    return sorted(hops, key=lambda d: hops[d] == d) + [c]
+
+
+def asks_at(src, dst, T, topo):
+    return 16 * peers(dst, T, topo).index(src)
+
+
+def lands_at(src, dst, T, topo):
+    return 64 * (2 * len(T.cores) - 2 - peers(dst, T, topo).index(src))
+
+
 def relay_program(g, core, T, topo, src, dst):
-    n = len(T.cores)
-    r, q = T.rank_of(src), T.rank_of(dst)
     rid, pid = topo.addr(dst, core)
-    m = bits(topo.engines(core, dst)[:NE])
-    sl = (r - q - 1) % n
-    g.wait_ge(T.sem.rq, NE)
-    g.remote_dma(T.req[:, 16 * sl:16 * sl + 16], T.req[:, 0:16], T.sem.rq, T.sem.snt, pid, rid, m)
-    g.wait_ge(T.sem.rp, NE)
-    g.remote_dma(T.land[:, 64 * r:64 * r + 64], T.land[:, 0:64], T.sem.rp, T.sem.snt, pid, rid, m)
-    g.wait_ge(T.sem.snt, 2 * NE)
+    es = topo.engines(core, dst)[:OPT["ne"]]
+    got = len(engine_sets(src, T, topo)[dst])
+    c = asks_at(src, dst, T, topo)
+    g.wait_ge(T.sem.rq, got)
+    g.remote_dma(T.qv[:, c:c + 16], T.qv[:, 0:16], T.sem.rq, T.sem.snt, pid, rid, bits(es))
+    g.wait_ge(T.sem.rp, got)
+    c = lands_at(src, dst, T, topo)
+    g.remote_dma(T.land[:, c:c + 64], T.land[:, 0:64], T.sem.rp2, T.sem.snt, pid, rid, bits(es))
+    g.wait_ge(T.sem.snt, 2 * len(es))
 
 
 def rank_program(g, core, T, topo):
@@ -99,9 +147,10 @@ def rank_program(g, core, T, topo):
     n = len(T.cores)
     A, F = AluOpType, ActivationFunctionType
     Q = {"v": g.vector, "a": g.scalar, "p": g.tensor, "g": g, "s": g.sync}
+    V = g.vector
     cnt = {"v": 0, "a": 0, "p": 0, "g": 0}
     waited = {e: {} for e in Q}
-    wr, rd = {}, {}
+    log = {}
 
     def wait(e, tok):
         if waited[e].get(tok[0], 0) < tok[1]:
@@ -109,29 +158,25 @@ def rank_program(g, core, T, topo):
             waited[e][tok[0]] = tok[1]
 
     def ap(r):
-        return T[r[0]][:, r[1]:r[2]]
-
-    def span(r):
-        return (r[0], 0, 512) if r[0].startswith("ps") else r
+        return T[r[0]][:, r[1]:r[2]:r[3]] if len(r) > 3 else T[r[0]][:, r[1]:r[2]]
 
     def order(e, reads, writes):
         need = {}
-        for r, logs in [(x, (wr,)) for x in reads] + [(x, (wr, rd)) for x in writes]:
-            nm, lo, hi = span(r)
-            for log in logs:
-                for (l2, h2, tok) in log.get(nm, []):
-                    if l2 < hi and lo < h2 and not (e == "p" and tok[0] == "p"):
-                        need[tok[0]] = max(need.get(tok[0], 0), tok[1])
+        for r, w in [(x, False) for x in reads] + [(x, True) for x in writes]:
+            for (r2, w2, tok) in log.get(r[0], []):
+                if e == "p" and tok[0] == "p":
+                    continue
+                bank = r[0].startswith("ps") and tok[0] != e
+                apart = len(r) > 3 and r[3:] == r2[3:] and (r[1] - r2[1]) % r[3] != 0
+                apart = apart or (len(r) > 4 and len(r2) > 4 and r[4] != r2[4])
+                if bank or ((w or w2) and r2[1] < r[2] and r[1] < r2[2] and not apart):
+                    need[tok[0]] = max(need.get(tok[0], 0), tok[1])
         for k in need:
             wait(e, (k, need[k]))
 
     def note(tok, reads, writes):
-        for r in reads:
-            nm, lo, hi = span(r)
-            rd.setdefault(nm, []).append((lo, hi, tok))
-        for r in writes:
-            nm, lo, hi = span(r)
-            wr.setdefault(nm, []).append((lo, hi, tok))
+        for r, w in [(x, False) for x in reads] + [(x, True) for x in writes]:
+            log.setdefault(r[0], []).append((r, w, tok))
 
     def op(e, fn, reads, writes):
         order(e, reads, writes)
@@ -140,80 +185,65 @@ def rank_program(g, core, T, topo):
         ins.then_inc(T.sem[e], 1)
         note((e, cnt[e]), reads, writes)
 
+    def val(s):
+        return ap(s) if isinstance(s, tuple) else s
+
     def ts(out, in0, s1, op0, s2=None, op1=None):
+        rs = [in0] + [s for s in (s1, s2) if isinstance(s, tuple)]
         if op1 is None:
-            op("v", lambda: g.vector.tensor_scalar(ap(out), ap(in0), s1, None, op0), [in0], [out])
+            op("v", lambda: V.tensor_scalar(ap(out), ap(in0), val(s1), None, op0), rs, [out])
         else:
-            op("v", lambda: g.vector.tensor_scalar(ap(out), ap(in0), s1, s2, op0, op1), [in0], [out])
+            op("v", lambda: V.tensor_scalar(ap(out), ap(in0), val(s1), val(s2), op0, op1), rs, [out])
 
     def tt(out, a, b, o):
-        op("v", lambda: g.vector.tensor_tensor(ap(out), ap(a), ap(b), o), [a, b], [out])
+        op("v", lambda: V.tensor_tensor(ap(out), ap(a), ap(b), o), [a, b], [out])
 
     def cp(out, a):
-        op("v", lambda: g.vector.tensor_copy(ap(out), ap(a)), [a], [out])
+        op("v", lambda: V.tensor_copy(ap(out), ap(a)), [a], [out])
 
     def fill(out, c):
-        op("v", lambda: g.vector.memset(ap(out), c), [], [out])
+        op("v", lambda: V.memset(ap(out), c), [], [out])
+
+    def act(out, a, col=None):
+        if col is None:
+            op("a", lambda: g.scalar.activation(ap(out), ap(a), F.Copy), [a], [out])
+        else:
+            op("a", lambda: g.scalar.activation(ap(out), ap(a), F.Identity, bias=ap(col)), [a, col], [out])
 
     def gather(e, out, win, off):
         if e == "v":
-            op("v", lambda: g.vector.tensor_copy(ap(out), ap(win).indirect(ap(off))), [win, off], [out])
+            op("v", lambda: V.tensor_copy(ap(out), ap(win).indirect(ap(off))), [win, off], [out])
         else:
             op("a", lambda: g.scalar.activation(ap(out), ap(win).indirect(ap(off)), F.Copy), [win, off], [out])
 
     def scatter(e, win, off, src):
         if e == "v":
-            op("v", lambda: g.vector.tensor_copy(ap(win).indirect(ap(off)), ap(src)), [src, off], [win])
+            op("v", lambda: V.tensor_copy(ap(win).indirect(ap(off)), ap(src)), [src, off], [win])
         else:
             op("a", lambda: g.scalar.activation(ap(win).indirect(ap(off)), ap(src), F.Silu), [src, off], [win])
 
-    def mm(out_ap, out, terms):
-        reads = [r for t in terms for r in t[2]]
-
+    def mm(out, terms):
         def fn():
             for i, t in enumerate(terms):
-                ins = g.tensor.matmul(out_ap, t[0], t[1], i == 0, i == len(terms) - 1)
+                ins = g.tensor.matmul(ap(out), ap(t[0]), ap(t[1]), i == 0, i == len(terms) - 1)
             return ins
-        op("p", fn, reads, [out])
+        op("p", fn, [r for t in terms for r in t], [out])
 
-    def pack(out, fields, nine=False):
-        terms = []
-        for s, rs in enumerate(fields):
-            wt = ("w", 128 * (s + 4 * nine), 128 * (s + 4 * nine) + 128)
-            for r in rs:
-                terms.append((ap(wt), ap(r), [wt, r]))
-        mm(ap(out), out, terms)
+    def sub(r, a, b, *st):
+        return (r[0], r[1] + a, r[1] + b) + st
 
-    def sub(r, a, b):
-        return (r[0], r[1] + a, r[1] + b)
+    def iota(out, pat, base, cm):
+        if out[0] == "yi":
+            op("g", lambda: g.iota(ap(out), pat, base, cm), [], [out])
+        else:
+            op("g", lambda: g.iota(ap(out), pat, base, cm, allow_small_or_imprecise_dtypes=True), [], [out])
 
-    def pack_cand(out, srcs, nine=False, blocks=range(4)):
-        for j, q in enumerate(blocks):
-            pack(sub(out, 64 * j, 64 * j + 64),
-                 [[sub(r, 256 * q + 64 * s, 256 * q + 64 * s + 64) for r in srcs] for s in range(4)], nine)
+    def widen(out, a):
+        op("g", lambda: g.affine_select(ap(out), ap(a), [[0, a[2] - a[1]]], A.is_gt, 0.0, 1, 0), [a], [out])
 
-    def empty_bits(si, b):
-        ts(b, si, 1, A.logical_shift_right, M21, A.bitwise_and)
-        yield
-        ts(b, b, -1.0, A.mult, float(32 * ONES), A.add)
-        yield
-        ts(b, b, 5, A.logical_shift_right, ONES, A.bitwise_and)
-        yield
-
-    def fitch(src, a, b):
-        if src != a:
-            cp(a, src)
-            yield
-        yield from empty_bits(a, b)
-        ts(b, b, 21.0, A.mult)
-        yield
-        tt(b, b, src, A.add)
-        yield
-
-    def unpack(b, outs):
-        for s, r in enumerate(outs):
-            ts(r, b, 6 * s + 1, A.logical_shift_right, 21, A.bitwise_and)
-            yield
+    def load(e, sem, out, src):
+        Q[e].dma_start(ap(out), src).then_inc(T.sem[sem], 16)
+        note((sem, 16), [], [out])
 
     def late(k, gen):
         for _ in range(k):
@@ -227,328 +257,465 @@ def rank_program(g, core, T, topo):
                 if next(x, "end") == "end":
                     gens.remove(x)
 
-    def load(e, sem, out, src):
-        Q[e].dma_start(ap(out), src).then_inc(T.sem[sem], 16)
-        note((sem, 16), [], [out])
-
-    def U(a, b):
-        return ("u", a - 4096, b - 4096)
-
-    def X(a, b):
-        return ("x", a, b)
-
-    def O(a, b):
-        return ("o", a - 6144, b - 6144)
-
-    def OFF(d, side, a, b):
-        c = (2 * (S[d] - 4096) + side * (S[d + 1] - S[d])) // 16
-        return ("off", c + a // 16, c + b // 16)
-
-    def C(d, side, a, b):
-        nd = S[d + 1] - S[d]
-        nm, base = {1: ("c1", 0), 2: ("c2", 0), 3: ("c3", 0), 4: ("c3", 1024), 5: ("c3", 1536)}[d]
-        return (nm, base + side * nd + a, base + side * nd + b)
-
-    def QO(i):
-        return ("qo", 64 * i, 64 * i + 64)
-
-    def QI(i):
-        return ("qi", 64 * i, 64 * i + 64)
-
-    def GQ(i):
-        return ("gq", 1024 * i, 1024 * i + 1024)
-
     def PS(b, a, c):
         return ("ps%d" % b, a, c)
 
-    load("a", "dri", ("ri", 0, 248), T.right[:])
+    def CF(a, b=None):
+        return ("cf", a, a + 1 if b is None else b)
+
+    def YI(a, b=None):
+        return ("yi", a, a + 1 if b is None else b)
+
+    def G(d, a, b):
+        return ("big", PAD + S[d] - S[1] + a, PAD + S[d] - S[1] + b)
+
+    def OFF(d, side, a, b):
+        c = 120 * side + (S[d] - S[2]) // 16
+        return ("off", c + a // 16, c + b // 16)
+
+    def H(d, side, a, b):
+        c = B[d] + side * (512 >> d)
+        return ("u", c + a, c + b)
+
+    def QO(i, a=0, b=64):
+        return ("qo", 64 * i + a, 64 * i + b)
+
+    def QI(i, a=0, b=64):
+        return ("qi", 64 * i + a, 64 * i + b)
+
     load("s", "dli", ("li", 0, 248), T.left[:])
-    NL = 4
-    LW = 4096 // NL
-    for j in range(NL):
-        load("s", "dl%d" % j, ("lf", LW * j, LW * j + LW), T.leaf[:, LW * j:LW * j + LW])
+    load("a", "dri", ("ri", 0, 248), T.right[:])
     load("s", "dcl", ("cl", 0, 64), T.clade[:])
-    load("s", "ded", ("ed", 0, 64), T.edge[:])
-    load("s", "drq", ("req", 48, 64), T.clade[:, 16 * me:16 * me + 16])
+    load("a", "ded", ("qv", 64, 128), T.edge[:])
+    load("s", "drq", ("qv", 48, 64), T.clade[:, 16 * me:16 * me + 16])
+    for j in range(2):
+        load("s", "dl%d" % j, ("lf", 2048 * j, 2048 * j + 2048), T.leaf[:, 2048 * j:2048 * j + 2048])
 
-    def iota(out, pat, base, cm, fl=True):
-        if fl:
-            op("g", lambda: g.iota(ap(out), pat, base, cm, allow_small_or_imprecise_dtypes=True), [], [out])
-        else:
-            op("g", lambda: g.iota(ap(out), pat, base, cm), [], [out])
+    OH, GRP, BIAS, OFS = CF(0, 2), CF(16), CF(17, 20), CF(20)
+    XI = "xi"
+    iota(YI(0, 2), [[-1, 2]], 0, 1)
+    iota((XI, 0, 144), [[1, 144]], 0, -1)
+    iota(("ym", 0, 128), [[-16, 8], [0, 8], [-8, 2]], 0, 1)
+    iota(("ym", 128, 256), [[-16, 8], [0, 8], [8, 2]], 0, 1)
 
-    def narrow(a, b):
-        op("g", lambda: g.affine_select(ap(X(a, b)), ap(U(a, b)), [[0, b - a]], A.is_gt, 0.0, 1, 0), [U(a, b)], [X(a, b)])
+    fill(CF(24, 40), 4096.0)
+    fill(("big", PAD + 3968, 4096), 0.0)
+    op("a", lambda: g.scalar.activation(T.big[:, 0:PAD], T.cf[:, 24:40], F.Silu), [CF(24, 40)], [("big", 0, PAD)])
+    for d in (3, 2, 1):
+        ts(YI(33 + d), YI(0), d, A.logical_shift_right, 1, A.bitwise_and)
+    cp(CF(3), YI(36))
+    ts(CF(2), YI(36), -1.0, A.mult, 1.0, A.add)
+    ts(BIAS, YI(34, 37), 2 * BIG, A.mult, -BIG, A.add)
+    for c in range(OPT["junk"]):
+        act(("big", 4096 + 256 * c, 4352 + 256 * c), ("ym", 0, 256))
+    for i, (by, col) in enumerate(((0.0, 3), (-8.0, 3), (0.0, 2), (8.0, 2))):
+        ts(("wx", 128 * ((i + 2) % 4), 128 * ((i + 2) % 4) + 128), (XI, 0, 128), by, A.is_equal, CF(col), A.mult)
+    op("v", lambda: V.tensor_reduce(ap(CF(21)), ap(BIAS), AxisListType.X, A.add), [BIAS], [CF(21)])
 
-    iota(("xi", 0, 128), [[1, 128]], 0, -1)
-    iota(("yi", 0, 8), [[-16, 8]], 0, 1, False)
-    iota(("pay", 0, 1024), [[1, 1024]], PB, 0)
+    def sel(s):
+        ts(("ws", 128 * s, 128 * s + 128), ("ym", 128 * (s // 8), 128 * (s // 8) + 128), float(s), A.is_equal)
 
-    fill(("c1", 4096, 4112), 7.0)
-    fill(("c2", 2048, 2064), 21.0)
-    fill(O(S[5], S[6]), 21.0)
-    fill(("sl0", 4096, 4104), float(4096 + PB))
-    fill(("sl1", 2048, 2056), float(2048 + PB))
-    fill(("bm", 0, 144), 0.0)
-    fill(("gm", 0, 40), 0.0)
-    for s in range(8):
-        ts(("w", 128 * s, 128 * s + 128), ("xi", 0, 128), 0.0, A.is_equal, float(64 ** (s % 4) * (9 if s >= 4 else 1)), A.mult)
-    ts(("yi", 8, 16), ("yi", 0, 8), 4, A.arith_shift_right)
-    op("v", lambda: g.vector.tensor_scalar(T.bm[:, 16:144:16], T.yi[:, 0:8], 0.0, None, A.is_equal),
-       [("yi", 0, 8)], [("bm", 0, 144)])
-    op("v", lambda: g.vector.tensor_scalar(T.gm[:, 3:35:4], T.yi[:, 8:16], 0.0, None, A.is_equal),
-       [("yi", 8, 16)], [("gm", 0, 40)])
-
-    for d in range(1, 6):
-        for side in (1, 0):
-            nd = S[d + 1] - S[d]
-            ts(OFF(d, side, 0, nd), ("ri" if side else "li", (S[d] - 4096) // 16, (S[d + 1] - 4096) // 16),
-               float(S[d - 1]), A.subtract)
-    ts(("qo", 512, 520), ("ri", 240, 248), float(S[4]), A.subtract)
-    ts(("qo", 520, 528), ("li", 240, 248), float(S[4]), A.subtract)
+    for s in range(OPT["late"]):
+        sel(s)
+    ts(("lh", 0, 128), ("li", 0, 128), 2048.0, A.subtract)
+    ts(("lh", 128, 256), ("ri", 0, 128), 2048.0, A.subtract)
+    ts(OFS, CF(21), -0.5, A.mult, 2048.0 - 1.5 * BIG, A.add)
+    for s in range(OPT["late"], 16):
+        sel(s)
 
     hops = first_hops(core, T, topo)
-    dests = sorted(hops, key=lambda d: len(topo.engines(core, hops[d])))
-    used, masks = [], {}
-    for d in dests:
-        es = topo.engines(core, hops[d])
-        es = [e for e in (es if hops[d] == d else es[::-1]) if e not in used][:NE]
-        used += es
-        masks[d] = bits(es)
+    ring = peers(core, T, topo)
+    dests = ring[:-1]
+    masks = {d: bits(es) for d, es in engine_sets(core, T, topo).items()}
+    sent = sum(len(es) for es in engine_sets(core, T, topo).values())
+    come = {True: 0, False: 0}
+    for c in dests:
+        last = first_hops(c, T, topo)[core]
+        come[last == core] += len(engine_sets(c, T, topo)[core] if last == core else topo.engines(last, core)[:OPT["ne"]])
 
-    def send(src_of, dst_of, sem, reads):
-        order("g", reads, [])
+    def send(ds, src, dst, sem):
+        order("g", [src(d) for d in ds], [])
         trs = []
-        for d in dests:
+        for d in ds:
             rid, pid = topo.addr(hops[d], core)
+            o = dst(d) if hops[d] == d else sub(dst(d), -dst(d)[1], -dst(d)[1] + dst(d)[2] - dst(d)[1])
             trs.append(RemoteDMATransfer(dst_ids=[DstId(rid=rid, pnc=pid)], dma_engine_mask=masks[d], remote_sem=sem,
-                                         src=src_of(T.rank_of(d)), dst=dst_of(T.rank_of(d), hops[d] == d)))
+                                         src=ap(src(d)), dst=ap(o)))
         g.remote_dma_fused(trs, local_sem=T.sem.snt)
 
-    iota(("pay", 1024, 2048), [[1, 1024]], PB + 1024, 0)
-    send(lambda q: T.cl[:, 16 * q:16 * q + 16],
-         lambda q, direct: T.req[:, 16 * ((me - q - 1) % n) * direct:16 * ((me - q - 1) % n) * direct + 16],
-         T.sem.rq, [("cl", 0, 64)])
-    note(("rq", NE * (n - 1)), [], [("req", 0, 48)])
-    iota(("pay", 2048, 3072), [[1, 1024]], PB + 2048, 0)
-    iota(("pay", 3072, 4096), [[1, 1024]], PB + 3072, 0)
+    owners = [T.rank_of(c) for c in ring[::-1]]
+    iota(YI(40, 44), [[32, 2], [8, 2]], 0, 0)
+    for h in range(2):
+        iota(YI(44 + 2 * h, 46 + 2 * h), [[8, 2]], 16 * owners[2 * h], 0)
+    iota(("low", 0, 128), [[0, 2], [-1, 64]], 128, 0)
+    send(dests, lambda d: ("cl", 16 * T.rank_of(d), 16 * T.rank_of(d) + 16),
+         lambda d: ("qv", asks_at(core, d, T, topo), asks_at(core, d, T, topo) + 16), T.sem.rq)
+    note(("rq", come[True] + come[False]), [], [("qv", 0, 48)])
+    for c in range(4):
+        iota(("pay", 1024 * c, 1024 * c + 1024), [[-16, 4], [-1, 4], [0, 64]], 126 - 4 * c, 0)
+        if c % 2:
+            o = ("pay", 1024 * c - 1024, 1024 * c + 1024)
+            order("s", [("low", 0, 128)], [o])
+            g.sync.dma_start(T.pay[1:128:16, o[1]:o[2]], T.low[:, 0:128]).then_inc(T.sem["dp%d" % (c // 2)], 16)
+            note(("dp%d" % (c // 2), 16), [("low", 0, 128)], [o])
+    iota(("big", 4096 + 256 * OPT["junk"], 8192), [[0, 4096 - 256 * OPT["junk"]]], M21, 0)
+    iota(("kc", 0, 128), [[1, 8], [0, 16]], 0, 0)
 
-    SL0, SL1 = ("sl0", 0, 4096), ("sl1", 0, 2048)
-    at0, at1 = [0], [0]
+    QV = ("qp", 0, 128)
 
-    def slots(e, d, m):
-        at, half = ((at0, 2048), (at1, 1024))[d]
-        while m > 0 and at[0] < 2 * half:
-            a = at[0]
-            b = min(a + m, (a // half + 1) * half)
-            scatter(e, (SL0, SL1)[d], OFF(d + 1, 1 - a // half, a % half, a % half + b - a), ("pay", a, b))
-            m -= b - a
-            at[0] = b
+    def setup():
+        ts(YI(37), YI(0), 3, A.bitwise_and)
+        yield
+        ts(YI(33), YI(0), 1, A.bitwise_and)
+        yield
+        ts(YI(16, 18), YI(0, 2), 15, A.bitwise_and)
+        yield
+        ts(YI(32), YI(0), 4, A.logical_shift_right)
+        yield
+        ts(OH, YI(16, 18), 0.0, A.is_equal)
+        yield
+        cp(GRP, YI(32))
+        yield
+        ts(CF(22), YI(33), 63.0, A.mult, 1.0, A.add)
+        yield
+        ts(CF(23), YI(34), 9.0 * 4095, A.mult, 9.0, A.add)
+        yield
+        cp(CF(46), YI(37))
+        yield
+        ts(CF(40), YI(37), -1.0, A.mult, 3.0, A.add)
+        yield
+        tt(CF(41), CF(22), CF(23), A.mult)
+        yield
+        ts(CF(47), YI(36), 4.0, A.mult, CF(46), A.add)
+        yield
+        ts(("wp", 0, 136), ("xi", 0, 136), CF(40), A.is_equal, CF(41), A.mult)
+        yield
+        ts(CF(24), YI(35), 16.0, A.mult, CF(47), A.add)
+        yield
+        for h in range(2):
+            ts(CF(25 + h), YI(35), 16.0 * (owners[2 * h + 1] - owners[2 * h]), A.mult, CF(47), A.add)
+            yield
+        ts(CF(44), YI(37), 8.0, A.mult, GRP, A.add)
+        yield
+        ts(("pl", 0, 4), YI(40, 44), CF(24), A.add)
+        yield
+        for h in range(2):
+            ts(("pl", 4 + 2 * h, 6 + 2 * h), YI(44 + 2 * h, 46 + 2 * h), CF(25 + h), A.add)
+            yield
+        ts(("bm", 0, 144), ("xi", 0, 144), 16.0, A.is_equal, CF(0), A.mult)
+        yield
 
-    slots("a", 0, 512)
-    slots("v", 1, 512)
-    for j in range(NL - 1):
-        ts(X(LW * j, LW * j + LW), ("lf", LW * j, LW * j + LW), 9.0, A.mult)
+    def setup2():
+        ts(("wi", 0, 128), ("xi", 0, 128), 0.0, A.is_equal)
+        yield
+        for d in range(1, 6):
+            ts(("sb", 128 * d - 128, 128 * d), QV, float(S[d]), A.is_ge, 2.0 ** -d, A.mult)
+            yield
+        mm(PS(7, 0, 128), [(("wi", 0, 128), ("sb", 128 * d, 128 * d + 128)) for d in range(5)])
+        ts(("bt", 0, 144), ("xi", 0, 144), 15.0, A.is_equal, CF(1), A.mult)
+        yield
+        ts(("bh", 0, 144), ("bm", 0, 144), 64.0, A.mult)
+        yield
+        tt(("qi", 0, 128), PS(6, 0, 128), QV, A.min)
+        yield
+        tt(("bh", 0, 144), ("bh", 0, 144), ("bt", 0, 144), A.add)
+        yield
+        ts(("m2", 0, 128), PS(7, 0, 128), -1.0, A.add)
+        yield
+        cp(("qo", 128, 256), ("qi", 0, 128))
+        yield
+
+    def setup3():
+        cp(CF(45), YI(0))
+        ts(("kc", 0, 128), ("kc", 0, 128), 0.125, A.mult)
+        ts(("gm", 0, 32), ("xi", 0, 32), CF(45), A.add, CF(44), A.is_equal)
+
+    early, more = setup(), setup2()
+
+    def some(k, gen=early):
+        for _ in range(k):
+            if next(gen, "end") != "end":
+                yield
+
+    def asked(h):
+        gather("v", sub(QV, 64 * h, 64 * h + 64), ("qv", 64 * h, 64 * h + 64), ("pl", 4 * h, 4 * h + 4))
+        ts(QO(h), sub(QV, 64 * h, 64 * h + 64), float(S[1] - PAD), A.subtract)
+
+    for i in range(2):
+        mm(PS(6 + i, 256, 384), [(("wx", 256 * i + 128 * side, 256 * i + 128 * side + 128), ("lh", 128 * side, 128 * side + 128))
+                                 for side in (0, 1)])
+        cp(("lx", 128 * i, 128 * i + 128), PS(6 + i, 256, 384))
+    ts(("off", 120, 240), ("ri", 128, 248), float(S[1] - PAD), A.subtract)
+    ts(("off", 0, 120), ("li", 128, 248), float(S[1] - PAD), A.subtract)
+    for s in range(16):
+        mm(PS(s // 2, 128 * (s % 2), 128 * (s % 2) + 128),
+           [(("ws", 128 * s, 128 * s + 128), ("lx", 128 * (s // 8), 128 * (s // 8) + 128))])
+    for s in range(16):
+        o, src = ("big", PAD + s, PAD + 2048, 16), PS(s // 2, 128 * (s % 2), 128 * (s % 2) + 128)
+        if OPT["ev"][s // 2] == "a":
+            act(o, src, OFS)
+        else:
+            ts(o, src, OFS, A.add)
+            if s % 2:
+                run(some(2))
+
+    for d, cuts, k in ((2, (0, 128, 384, 704, 1024), 4), (3, (0, 128, 320, 512), 4), (4, (0, 96, 256), 3)):
+        win = ("big", 0, G(d, 0, 0)[1])
+        run(some(k))
+        for a, m in [(x, y - x) for x, y in zip(cuts, cuts[1:])]:
+            t, col = ("xa", a, a + m), CF(15 + d)
+            op("a", lambda: g.scalar.activation(ap(t), ap(win).indirect(ap(OFF(d, 1, a, a + m))), F.Identity, bias=ap(col)),
+               [win, OFF(d, 1, a, a + m), col], [t])
+            op("v", lambda: V.tensor_tensor(ap(G(d, a, a + m)), ap(win).indirect(ap(OFF(d, 0, a, a + m))), ap(t), A.max),
+               [win, OFF(d, 0, a, a + m), t], [G(d, a, a + m)])
+    win = ("big", 0, G(5, 0, 0)[1])
+    run(early)
+    for side in (0, 1):
+        gather("v", ("pi", side, 256, 2), win, OFF(5, side, 0, 128))
+    gather("a", G(5, 0, 128), win, OFF(5, 0, 0, 128))
 
     LF = ("lf", 0, 4096)
-    CH = (256, 256, 512, 512, 256, 256)
-    lo = 0
-    for j, m in enumerate(CH):
+
+    def leaves(e, a, b):
+        if b > a:
+            gather(e, ("c1", a, b), LF, ("pi", a // 16, b // 16))
+
+    def words(c):
         for side in (0, 1):
-            gather("v" if j == 0 else "a", C(1, side, lo, lo + m), LF, OFF(1, side, lo, lo + m))
-        lo += m
+            mm(PS(c, 128 * side, 128 * side + 128),
+               [(("wp", 3 - k, 131 - k), ("c1", 1024 * c + 256 * k + side, 1024 * c + 256 * k + 256, 2)) for k in range(4)])
 
-    def level1(j, lo, hi):
-        wd = (hi - lo) // 4
-        for side in (0, 1):
-            pack(PS(j, wd * side, wd * side + wd),
-                 [[C(1, side, lo + wd * s, lo + wd * s + wd)] for s in range(4)], True)
-        t = ("dn", lo // 2, hi // 2)
-        a, b = ("ta", lo // 4, hi // 4), ("tb", lo // 4, hi // 4)
-        cp(t, PS(j, 0, 2 * wd))
+    def empty_bits(a, b):
+        ts(b, a, 1, A.logical_shift_right, M21, A.bitwise_and)
         yield
-        ts(t, t, M21, A.bitwise_and)
+        ts(b, b, -1.0, A.mult, float(32 * ONES), A.add)
         yield
-        tt(a, sub(t, 0, wd), sub(t, wd, 2 * wd), A.add)
+        ts(b, b, 5, A.logical_shift_right, ONES, A.bitwise_and)
         yield
-        yield from fitch(a, a, b)
-        yield from unpack(b, [U(4096 + lo + wd * s, 4096 + lo + wd * s + wd) for s in range(4)])
 
-    lo = 0
-    for j in range(0, len(CH), 2):
-        m, m2 = CH[j], CH[j + 1]
-        run(level1(j % 4, lo, lo + m), level1((j + 1) % 4, lo + m, lo + m + m2))
-        if j == 0:
-            ts(X(4096 - LW, 4096), ("lf", 4096 - LW, 4096), 9.0, A.mult)
-            ed = ("ed", 0, 64)
-            ts(QO(0), ed, 4096.0, A.min)
-            cp(QO(1), ed)
-            ts(QI(0), ed, 4096.0, A.subtract)
-            ts(QI(1), ed, 6144.0, A.subtract)
-        narrow(4096 + lo, 4096 + lo + m + m2)
-        lo += m + m2
-    slots("a", 0, 1536)
+    def fitch(a, b, outs, spare=None, src=None):
+        yield from empty_bits(a, b)
+        t = spare or b
+        ts(t, b, 21.0, A.mult)
+        yield
+        tt(b, t, src or a, A.add)
+        yield
+        for s, out in enumerate(outs):
+            ts(out, sub(b, s, b[2] - b[1], len(outs)), 1, A.logical_shift_right, M21, A.bitwise_and)
+            yield
 
-    def kids(e, d, lo, hi):
-        win = U(S[d - 1], S[d]) if e == "v" else X(S[d - 1], S[d])
-        if hi - lo == S[d + 1] - S[d]:
-            gather(e, sub(C(d, 0, 0, 0), 0, 2 * hi), win, sub(OFF(d, 0, 0, 0), 0, hi // 8))
+    def up(d, lo, hi, i):
+        a, b = ("ta", 256 * i, 256 * i + hi - lo), ("tb", 256 * i, 256 * i + hi - lo)
+        tt(a, H(d - 1, 0, lo, hi), H(d - 1, 1, lo, hi), A.add)
+        yield
+        outs = [H(d, s, lo // 2, hi // 2) for s in (0, 1)] if d < 5 else [H(d, 0, lo, hi)]
+        yield from fitch(a, b, outs, PS(4 + i, 0, hi - lo) if hi - lo > 32 else None)
+
+    def level1(c, i):
+        w = ("tb", 256 * i, 256 * i + 256)
+        cp(w, PS(c, 0, 256))
+        yield
+        for s in (0, 1):
+            ts(H(0, s, 128 * c, 128 * c + 128), sub(w, 128 * s, 128 * s + 128), M21, A.bitwise_and)
+            yield
+        yield from up(1, 128 * c, 128 * c + 128, i)
+
+    def table(cls, d):
+        src, sem = (("uf", "us", "af")[cls], B[d], B[d + 1]), "t%d%d" % (cls, d)
+        out = ("big", 4 * B[d], 4 * B[d + 1], 1, cls)
+        order("s", [src], [out])
+        g.sync.dma_start(T.big[cls:128:4, out[1]:out[2]], ap(src)).then_inc(T.sem[sem], 16)
+        note((sem, 16), [src], [out])
+
+    def level_out(d, cls=0):
+        if d < 5:
+            for s in (0, 1):
+                widen((("uf", "us")[cls], B[d] + s, B[d + 1], 2), H(d, s ^ cls, 0, 512 >> d))
         else:
-            for side in (0, 1):
-                gather(e, C(d, side, lo, hi), win, OFF(d, side, lo, hi))
+            widen(("uf", B[d], B[d + 1]), H(d, 0, 0, 32))
+        table(cls, d)
 
-    def up_pack(d, lo, hi, k, bank):
-        wd = (hi - lo) // k
-        pack(PS(bank, 0, wd), [[C(d, side, lo + wd * s, lo + wd * s + wd) for side in (0, 1)] for s in range(k)])
+    def to_list(out, src, wt="bm"):
+        w = src[2] - src[1]
+        mm(out, [((wt, 16 - s, 144 - s), sub(src, s, w, 16)) for s in range(16)])
 
-    def up(d, lo, hi, k, bank, t0):
-        wd = (hi - lo) // k
-        a, b = ("ta", t0, t0 + wd), ("tb", t0, t0 + wd)
-        yield from fitch(PS(bank, 0, wd), a, b)
-        yield from unpack(b, [U(S[d] + lo + wd * s, S[d] + lo + wd * s + wd) for s in range(k)])
+    POS = ("pos", 0, 4096)
 
-    GS = ("gs", 0, 1024)
+    def spread(e, a, b):
+        scatter(e, POS, ("pi", a // 16, b // 16), ("pay", a, b))
 
-    def to_list(bank):
-        mm(T["ps%d" % bank][:, 0:64], PS(bank, 0, 64),
-           [(T.bm[:, 16 - s:144 - s], T.gs[:, s:1024:16], [("bm", 0, 144), GS]) for s in range(16)])
+    def leftmost(h):
+        x = ("xa", 1024 * h, 1024 * h + 1024)
+        gather("a", x, ("big", 0, 4096), QO(h))
+        to_list(PS(6, 64 * h, 64 * h + 64), x)
 
-    for i in range(4):
-        kids("v" if i < 2 else "a", 2, 256 * i, 256 * i + 256)
-        up_pack(2, 256 * i, 256 * i + 256, 4, 4 + i)
-    for i in (0, 2):
-        run(up(2, 256 * i, 256 * i + 256, 4, 4 + i, 512 + 64 * i), up(2, 256 * i + 256, 256 * i + 512, 4, 5 + i, 576 + 64 * i))
-        narrow(S[2] + 256 * i, S[2] + 256 * i + 512)
-    for i in range(2):
-        kids("v", 3, 256 * i, 256 * i + 256)
-        up_pack(3, 256 * i, 256 * i + 256, 4, i)
-    slots("a", 0, 4096)
-    gather("a", GS, ("sl0", 0, 4104), QO(0))
-    cp(QO(2), ("req", 0, 64))
-    run(up(3, 0, 256, 4, 0, 0), late(3, up(3, 256, 512, 4, 1, 64)))
-    narrow(S[3], S[4])
-    kids("v", 4, 0, 256)
-    up_pack(4, 0, 256, 4, 2)
-    slots("v", 1, 128)
-    run(up(4, 0, 256, 4, 2, 128))
-    narrow(S[4], S[5])
-    kids("v", 5, 0, 128)
-    up_pack(5, 0, 128, 2, 4)
+    for c in range(4):
+        m = 1024 * c + OPT["lv"][c]
+        leaves("v", 1024 * c, m)
+        leaves("a", m, 1024 * c + 1024)
+        words(c)
+        if c == 0:
+            asked(1)
+    leftmost(1)
+    spread("a", 0, OPT["llc"])
 
-    scatter("v", O(S[4], S[5]), ("qo", 512, 528), ("c3", 1536, 1792))
+    def clades():
+        asked(0)
+        leftmost(0)
+        spread("a", OPT["llc"], 4096)
+        yield
 
-    def down_pack(d, lo, hi, bank):
-        h = (hi - lo) // 2
-        pack(PS(bank, 0, h), [[O(S[d + 1] + lo + h * (s % 2), S[d + 1] + lo + h * (s % 2) + h),
-                               C(d + 1, 1 - s // 2, lo + h * (s % 2), lo + h * (s % 2) + h)] for s in range(4)])
+    def now(k):
+        return late(OPT["a0"][1], clades()) if OPT["a0"][0] == k else ()
 
-    def down(d, lo, hi, bank, t0):
-        h, npar = (hi - lo) // 2, S[d + 2] - S[d + 1]
-        a, b = ("ta", t0, t0 + h), ("tb", t0, t0 + h)
-        yield from fitch(PS(bank, 0, h), a, b)
-        c0 = [npar * (s // 2) + lo + h * (s % 2) for s in range(4)]
-        yield from unpack(b, [("dn", c, c + h) for c in c0])
+    run(level1(0, 0), late(2, level1(1, 1)), iter(now(0)))
+    run(level1(2, 0), late(2, level1(3, 1)), iter(now(1)))
+    level_out(0)
+    level_out(0, 1)
+    level_out(1)
+    run(up(2, 0, 128, 0), late(2, up(2, 128, 256, 1)), iter(now(2)))
+    level_out(1, 1)
+    level_out(2)
+    run(up(3, 0, 64, 0), late(2, up(3, 64, 128, 1)))
+    level_out(3)
+    run(up(4, 0, 64, 0), some(8, more))
+    level_out(4)
 
-    def down_scatter(d):
-        npar = S[d + 2] - S[d + 1]
-        scatter("v", O(S[d], S[d + 1]), sub(OFF(d + 1, 0, 0, 0), 0, npar // 8), ("dn", 0, 2 * npar))
-
-    def step(bank, i_s, i_t, mask, prev, o_sib, o_next, cap):
-        ts(QI(i_s), PS(bank, 0, 64), float(PB), A.subtract)
-        ts(QI(i_t), QI(i_s), mask, A.bitwise_and)
-        cp(QO(o_sib), QI(i_s))
-        tt(QI(i_t), QI(i_t), prev, A.max)
-        ts(QO(o_next), QI(i_t), float(cap), A.min)
-
-    XA = X(0, S[6])
-    down_pack(3, 0, 256, 1)
-    to_list(6)
-    run(up(5, 0, 128, 2, 4, 192), late(3, down(3, 0, 256, 1, 256)))
-    narrow(S[5], S[6])
-    iota(("kc", 0, 128), [[1, 2], [0, 16], [2, 4]], 0, 0)
-    slots("a", 1, 2048)
-    down_scatter(3)
-    down_pack(2, 0, 256, 2)
-    down_pack(2, 256, 512, 4)
-    step(6, 2, 3, 2047, QI(0), 4, 5, 2048)
-    gather("a", GQ(1), XA, QO(2))
-    pack_cand(PS(0, 0, 256), [GQ(1)])
-    gather("a", GS, ("sl1", 0, 2056), QO(5))
-    to_list(7)
-    gather("a", GQ(2), ("c1", 0, 4112), QO(4))
-    pack_cand(PS(1, 0, 256), [GQ(2)], True)
-    gather("a", GQ(0), XA, QO(1))
-    pack_cand(PS(1, 256, 512), [GQ(0)])
-    run(down(2, 0, 256, 2, 384), late(3, down(2, 256, 512, 4, 512)))
-    down_scatter(2)
-    step(7, 4, 5, 1023, QI(1), 6, 7, 1919)
-    for h in range(4):
-        gather("a", sub(GQ(3), 256 * h, 256 * h + 256), ("c2", 0, 2064), sub(QO(6), 16 * h, 16 * h + 16))
-        gather("a", sub(GQ(4), 256 * h, 256 * h + 256), ("o", 0, 1920), sub(QO(7), 16 * h, 16 * h + 16))
-
-    CLM, PR = ("pre", 512, 768), ("pre", 0, 512)
-    cp(CLM, PS(0, 0, 256))
-    ts(("kc", 0, 128), ("kc", 0, 128), 0.125, A.mult)
-    ts(("snd", 0, 192), sub(CLM, 0, 192), M21, A.bitwise_and)
-    ts(("land", 64 * me, 64 * me + 64), sub(CLM, 192, 256), M21, A.bitwise_and)
-    send(lambda q: T.snd[:, 64 * ((q - me - 1) % n):64 * ((q - me - 1) % n) + 64],
-         lambda q, direct: T.land[:, 64 * me * direct:64 * me * direct + 64],
-         T.sem.rp, [("snd", 0, 192)])
-    note(("rp", NE * (n - 1)), [], [("land", 64 * q, 64 * q + 64) for q in range(n) if q != me])
-    cp(PR, PS(1, 0, 512))
-    ts(PR, PR, M21, A.bitwise_and)
-
-    def chain(q0, q1, bank):
-        lo, hi = 64 * q0, 64 * q1
-        wd = hi - lo
-        pack_cand(PS(bank, 0, wd), [GQ(4), GQ(3)], blocks=range(q0, q1))
-        a, b = ("ta", lo, hi), ("tb", lo, hi)
-        yield from fitch(PS(bank, 0, wd), a, b)
-        for i, nxt in enumerate((("pre", lo, hi), ("pre", 256 + lo, 256 + hi), ("land", lo, hi))):
-            ts(b, b, 1, A.logical_shift_right, M21, A.bitwise_and)
+    def sums(d, out, par, lo, hi):
+        for s in (0, 1):
+            tt(sub(out, 2 * lo + s, 2 * hi, 2), H(d, 1 - s, lo, hi), sub(par, lo, hi), A.add)
             yield
-            tt(a, b, nxt, A.add)
+
+    def down3():
+        for s in (0, 1):
+            cp(("o", s, 64, 2), H(4, 1 - s, 0, 32))
             yield
-            if i < 2:
-                yield from fitch(a, a, b)
+        yield from sums(3, ("ai", 256, 384), ("o", 0, 64), 0, 64)
+        yield from fitch(("ai", 256, 384), ("tb", 256, 384), [("o", 64, 192)], PS(5, 0, 128))
+
+    def down2(i):
+        yield from sums(2, ("ai", 0, 256), ("o", 64, 192), 64 * i, 64 * i + 64)
+        yield from fitch(("ai", 128 * i, 128 * i + 128), ("tb", 256 * i, 256 * i + 128), [("o", 192 + 128 * i, 320 + 128 * i)],
+                         PS(4 + i, 0, 128))
+        for s in (0, 1):
+            cp(("af", B[1] + 256 * i + s, B[1] + 256 * i + 256, 2), ("o", 192 + 128 * i, 320 + 128 * i))
+            yield
+
+    def outside(d, src):
+        for s in (0, 1):
+            widen(("af", B[d] + s, B[d + 1], 2), src)
+        table(2, d)
+
+    def lookup(e, h):
+        x = ("xh", 1024 * h, 1024 * h + 1024)
+        gather(e, x, POS, QO(2 + h))
+        to_list(PS(7 - h, 0, 64), x, "bh")
+
+    def index(h):
+        p = PS(7 - h, 0, 64)
+        t = QI(3 + h)
+        tt(t, p, ("m2", 64 * h, 64 * h + 64), A.mult)
+        yield
+        if not h:
+            ts(QO(4), t, 8192.0, A.add)
+            answer()
+            yield
+            return
+        ts(QO(6), t, 0.5, A.mult, 4095.75, A.add)
+        ts(QO(5), t, 8192.0, A.add)
+        yield
+
+    TAB = ("big", 0, 8192)
+
+    def moved(q, sem, cls, out, x):
+        order(q, [x], [out])
+        Q[q].dma_start(ap(out), T.xv[cls:128:4, x[1]:x[2]]).then_inc(T.sem[sem], 16)
+        note((sem, 16), [x], [out])
+
+    def operand(e, i, h):
+        x = ("xv", 1024 * (i + 1) + 512 * h, 1024 * (i + 1) + 512 * h + 512)
+        gather(e, x, TAB if i else ("big", 4096, 8192), QO(6 - i, 32 * h, 32 * h + 32))
+        for j, cls in enumerate((1, 0) if i else (2, 1)):
+            c = 256 * (2 * i + j) + 128 * h
+            moved("s", "d%d" % (4 * i + 2 * j + h), cls, ("so", c, c + 128), x)
+
+    def answer():
+        for h in range(2):
+            x, out = ("xv", 512 * h, 512 * h + 512), ("land", 128 * h, 128 * h + 128)
+            gather("a", x, TAB, QO(4, 32 * h, 32 * h + 32))
+            moved("s", "dc%d" % h, 0, out, x)
+        for ds in ([d for d in dests if hops[d] != d], [d for d in dests if hops[d] == d]):
+            send(ds, lambda d: ("land", 64 * ring.index(d), 64 * ring.index(d) + 64),
+                 lambda d: ("land", lands_at(core, d, T, topo), lands_at(core, d, T, topo) + 64), T.sem.rp)
+        note(("rp", come[True]), [], [("land", 256, 320)])
+        note(("rp2", come[False]), [], [("land", 320, 448)])
+
+    run(up(5, 0, 32, 0), down3(), late(2, more))
+    level_out(5)
+    for e, h in OPT["le"]:
+        if e == "a":
+            lookup(e, h)
+    outside(2, ("o", 64, 192))
+    outside(3, ("o", 0, 64))
+    for d in (2, 3, 4):
+        level_out(d, 1)
+    run(down2(0), late(2, down2(1)))
+    table(2, 1)
+    setup3()
+    for e, h in OPT["le"]:
+        if e == "v":
+            lookup(e, h)
+    for h in OPT["ix"]:
+        run(index(h))
+    for e, i, h in OPT["ops"]:
+        operand(e, i, h)
+
+    def walk(h):
+        lo, hi = 128 * h, 128 * h + 128
+        a, b, x = ("ta", lo, hi), ("tb", lo, hi), ("o", lo, hi)
+        spare = PS(1 + h, 128, 256)
+        for i in (1, 2, 3):
+            tt(a, x if i > 1 else ("so", lo, hi), ("so", 256 * i + lo, 256 * i + hi), A.add)
+            yield
+            yield from fitch(a, b, [x], spare)
+        tt(a, x, ("land", 192 + lo, 192 + hi), A.add)
+        yield
         yield from empty_bits(a, b)
         cp(("nzf", lo, hi), b)
-        for q in range(q0, q1):
-            op("p", lambda: g.tensor.matmul(T.ps7[0:64, 0:32], T.nzf[:, 64 * q:64 * q + 64], T.gm[:, 3 - q:35 - q], q == 0, q == 3),
-               [("nzf", 64 * q, 64 * q + 64), ("gm", 0, 40)], [PS(7, 0, 32)])
+        for j in (2 * h, 2 * h + 1):
+            q = owners[j]
+            op("p", lambda: g.tensor.matmul(T.ps7[0:64, 32 * q:32 * q + 32], T.nzf[:, 64 * j:64 * j + 64], T.gm[:, 0:32], True, True),
+               [("nzf", 64 * j, 64 * j + 64), ("gm", 0, 32)], [PS(7, 32 * q, 32 * q + 32)])
         yield
 
-    run(chain(0, 2, 2), late(2, chain(2, 4, 4)))
+    run(walk(0), late(OPT["lag"], walk(1)))
 
-    V = g.vector
-    op("v", lambda: V.tensor_copy(T.ki[0:64, 0:32], T.ps7[0:64, 0:32]), [PS(7, 0, 32)], [("ki", 0, 32)])
-    for s in range(4):
-        op("v", lambda: V.tensor_scalar(T.ki[0:64, 32 + 32 * s:64 + 32 * s], T.ki[0:64, 0:32], 6 * s, 63,
-                                        A.logical_shift_right, A.bitwise_and), [("ki", 0, 32)], [("ki", 32 + 32 * s, 64 + 32 * s)])
-    op("v", lambda: V.tensor_tensor(T.kf[0:64, 0:128], T.ki[0:64, 32:160], T.kc[0:64, :], A.add),
-       [("ki", 32, 160), ("kc", 0, 128)], [("kf", 0, 128)])
-    op("v", lambda: V.tensor_tensor(T.kf[0:64, 128:192], T.kf[0:64, 0:64], T.kf[0:64, 64:128], A.min),
-       [("kf", 0, 128)], [("kf", 128, 192)])
-    op("v", lambda: V.tensor_tensor(T.kf[0:64, 192:224], T.kf[0:64, 128:192:2], T.kf[0:64, 129:192:2], A.min),
-       [("kf", 128, 192)], [("kf", 192, 224)])
-    op("v", lambda: V.tensor_tensor(T.kb[0:64, 0:16], T.kf[0:64, 192:224:2], T.kf[0:64, 193:224:2], A.min),
-       [("kf", 192, 224)], [("kb", 0, 16)])
+    op("v", lambda: V.tensor_scalar(T.ki[0:64, :], T.ps7[0:64, 0:128], ONES / 262144.0, None, A.mult), [PS(7, 0, 128)], [("ki", 0, 128)])
+    op("v", lambda: V.tensor_scalar(T.ki[0:64, :], T.ki[0:64, :], 63, None, A.bitwise_and), [("ki", 0, 128)], [("ki", 0, 128)])
+    op("v", lambda: V.tensor_tensor(T.kf[0:64, 0:128], T.ki[0:64, :], T.kc[0:64, :], A.add),
+       [("ki", 0, 128), ("kc", 0, 128)], [("kf", 0, 128)])
+    a = 0
+    for w in (64, 32, 16):
+        out = T.kf[0:64, a + 2 * w:a + 3 * w] if w > 16 else T.kb[0:64, :]
+        op("v", lambda: V.tensor_tensor(out, T.kf[0:64, a:a + w], T.kf[0:64, a + w:a + 2 * w], A.min),
+           [("kf", a, a + 2 * w)], [("kf", a + 2 * w, a + 3 * w), ("kb", 0, 16)])
+        a += 2 * w
     for h in range(2):
-        mm(T.ps3[0:8, 64 * h:64 * h + 64], PS(3, 0, 128),
-           [(T.kb[0:64, 8 * h:8 * h + 8], T.w[0:64, 0:64], [("kb", 0, 16), ("w", 0, 128)])])
-    op("v", lambda: V.tensor_scalar(T.ei[0:8, 0:128], T.ps3[0:8, 0:128], 8.0, None, A.mult), [PS(3, 0, 128)], [("ei", 0, 128)])
-    op("v", lambda: V.tensor_scalar(T.ei[0:8, 128:256], T.ei[0:8, 0:128], 3, None, A.logical_shift_right),
-       [("ei", 0, 128)], [("ei", 128, 256)])
-    op("v", lambda: V.tensor_scalar(T.ei[0:8, 256:384], T.ei[0:8, 0:128], 7, None, A.bitwise_and),
-       [("ei", 0, 128)], [("ei", 256, 384)])
-    op("v", lambda: V.tensor_copy(T.ef[0:8, 0:256], T.ei[0:8, 128:384]), [("ei", 128, 384)], [("ef", 0, 256)])
-    order("s", [("ef", 0, 256)], [])
+        op("p", lambda: g.tensor.matmul(T.ps0[0:8, 64 * h:64 * h + 64], T.kb[0:64, 8 * h:8 * h + 8], T.wi[0:64, 0:64], True, True),
+           [("kb", 0, 16), ("wi", 0, 64)], [PS(0, 64 * h, 64 * h + 64)])
+    op("v", lambda: V.tensor_scalar(T.ei[0:8, :], T.ps0[0:8, 0:128], -0.4375, None, A.add), [PS(0, 0, 128)], [("ei", 0, 128)])
+    op("v", lambda: V.tensor_copy(T.ef[0:8, 0:128], T.ei[0:8, :]), [("ei", 0, 128)], [("ef", 0, 128)])
+    order("s", [("ef", 0, 128)], [])
     g.sync.dma_start(T.cost[:], T.ef[0:8, 0:128]).then_inc(T.sem.do1, 16)
-    order("a", [("ef", 0, 256)], [])
+    op("v", lambda: V.tensor_tensor(T.ef[0:8, 256:384], T.ps0[0:8, 0:128], T.ei[0:8, :], A.subtract),
+       [PS(0, 0, 128), ("ei", 0, 128)], [("ef", 256, 384)])
+    op("v", lambda: V.tensor_scalar(T.ef[0:8, 128:256], T.ef[0:8, 256:384], 8.0, None, A.mult),
+       [("ef", 256, 384)], [("ef", 128, 256)])
+    order("a", [("ef", 128, 256)], [])
     g.scalar.dma_start(T.first[:], T.ef[0:8, 128:256]).then_inc(T.sem.do2, 16)
 
     for e in cnt:
         wait("g", (e, cnt[e]))
-    wait("g", ("snt", 2 * NE * (n - 1)))
+    wait("g", ("snt", 2 * sent))
     wait("g", ("do1", 16))
     wait("g", ("do2", 16))

@@ -33,14 +33,14 @@ SCRATCH = {
     "xh": ("sbuf", [128, 2048], "bfloat16"),
     "xv": ("sbuf", [128, 5120], "float32"),
     "so": ("sbuf", [128, 1024], "float32"),
-    "u": ("sbuf", [128, 2048], "int32"),
+    "u": ("sbuf", [128, 2080], "int32"),
     "uf": ("sbuf", [128, 2048], "float32"),
     "us": ("sbuf", [128, 2048], "float32"),
     "af": ("sbuf", [128, 2048], "float32"),
     "ai": ("sbuf", [128, 512], "int32"),
     "o": ("sbuf", [128, 512], "int32"),
-    "ta": ("sbuf", [128, 512], "int32"),
-    "tb": ("sbuf", [128, 512], "int32"),
+    "ta": ("sbuf", [128, 1024], "int32"),
+    "tb": ("sbuf", [128, 1024], "int32"),
     "land": ("sbuf", [128, 448], "float32"),
     "qp": ("sbuf", [128, 128], "int32"),
     "pl": ("sbuf", [128, 8], "uint16"),
@@ -52,7 +52,7 @@ SCRATCH = {
     "yi": ("sbuf", [128, 72], "int32"),
     "cf": ("sbuf", [128, 72], "float32"),
     "wp": ("sbuf", [128, 136], "bfloat16"),
-    "we": ("sbuf", [128, 272], "float32"),
+    "we": ("sbuf", [128, 400], "float32"),
     "wi": ("sbuf", [128, 128], "bfloat16"),
     "wf": ("sbuf", [128, 64], "float32"),
     "bm": ("sbuf", [128, 144], "float32"),
@@ -69,11 +69,15 @@ for _b in range(8):
     SCRATCH["ps%d" % _b] = ("psum", [128, 512], "float32")
 
 SEMAPHORES = ["v", "a", "p", "g", "dl0", "dl1", "dli", "dri", "dcl", "ded", "drq", "do1", "do2",
-              "t00", "t01", "t02", "t03", "t04", "t05", "t10", "t11", "t12", "t13", "t14", "t21", "t22", "t23", "d0", "d1", "d2", "d3", "d4", "d5", "d6", "d7", "dp0", "dp1", "dc0", "dc1", "rq", "rp", "rp2", "snt"]
+              "t000", "t001", "t010", "t011", "t020", "t040", "t050", "t100", "t101", "t110", "t111", "t120", "t140",
+              "t210", "t211", "t220", "d0", "d1", "d2", "d3", "d4", "d5", "d6", "d7", "dp0", "dp1", "dj", "dc0", "dc1", "rq", "rp", "rp2", "snt"]
 
-OPT = {"lv": (512, 512, 1024, 512), "lag": 3, "ne": 8, "llc": 1024, "a0": (0, 8), "junk": 6, "late": 12,
-       "le": (("a", 0), ("v", 1)), "ix": (0, 1), "ev": "avavavav",
-       "ops": (("v", 0, 0), ("v", 0, 1), ("a", 1, 0), ("a", 1, 1))}
+OPT = {"lv": (512, 512, 512, 256), "lag": 3, "ne": 8, "llc": 768, "a0": 6, "junk": 5, "vj": 0, "pre": 1, "late": 12,
+       "ev": "avavavav", "pid": 1, "mid": (), "ic": 0, "pe": (), "pc": 0, "own": 0, "sg": 0, "wide": (1, 1, 0), "l1": 4,
+       "cuts": ((2, (0, 192, 576, 1024), 3), (3, (0, 160, 512), 3), (4, (0, 96, 256), 2)),
+       "tail": (("L", "a", 0, 0, 1024), ("T", 0), ("L", "v", 1, 0, 512), ("L", "a", 1, 512, 1024), ("T", 1),
+                ("I", 0), ("A", "a", 0), ("I", 1), ("O", "v", 0, 0), ("O", "a", 0, 1), ("O", "v", 1, 0), ("A", "a", 1),
+                ("O", "a", 1, 1))}
 
 
 def first_hops(src, T, topo):
@@ -96,12 +100,12 @@ def bits(engs):
     return sum(1 << e for e in engs)
 
 
-def engine_sets(src, T, topo):
+def engine_sets(src, T, topo, apart=False):
     hops = first_hops(src, T, topo)
     far = [d for d in hops if hops[d] == d]
     near = [d for d in hops if hops[d] != d]
     out = topo.engines(src, far[0])
-    rest = [e for e in topo.engines(src, hops[near[0]]) if e not in out]
+    rest = [e for e in topo.engines(src, hops[near[0]]) if apart or e not in out]
     sets = {}
     for ds, es in ((far, out), (near, rest)):
         k = len(es) // len(ds)
@@ -130,7 +134,7 @@ def relay_program(g, core, T, topo, src, dst):
     c = asks_at(src, dst, T, topo)
     g.wait_ge(T.sem.rq, got)
     g.remote_dma(T.qv[:, c:c + 16], T.qv[:, 0:16], T.sem.rq, T.sem.snt, pid, rid, bits(es))
-    g.wait_ge(T.sem.rp, got)
+    g.wait_ge(T.sem.rp, len(engine_sets(src, T, topo, True)[dst]))
     c = lands_at(src, dst, T, topo)
     g.remote_dma(T.land[:, c:c + 64], T.land[:, 0:64], T.sem.rp2, T.sem.snt, pid, rid, bits(es))
     g.wait_ge(T.sem.snt, 2 * len(es))
@@ -274,7 +278,7 @@ def rank_program(g, core, T, topo):
         return ("off", c + a // 16, c + b // 16)
 
     def H(d, side, a, b):
-        c = B[d] + side * (512 >> d)
+        c = 1024 * side + B[d] // 2 if d < 5 else 2048
         return ("u", c + a, c + b)
 
     def QO(i, a=0, b=64):
@@ -291,7 +295,7 @@ def rank_program(g, core, T, topo):
     for j in range(2):
         load("s", "dl%d" % j, ("lf", 2048 * j, 2048 * j + 2048), T.leaf[:, 2048 * j:2048 * j + 2048])
 
-    OH, GRP, BIAS, OFS = CF(0, 2), CF(16), CF(17, 20), CF(20)
+    OH, BIAS, OFS = CF(0, 2), CF(17, 20), CF(20)
     XI = "xi"
     iota(YI(0, 2), [[-1, 2]], 0, 1)
     iota((XI, 0, 144), [[1, 144]], 0, -1)
@@ -301,16 +305,40 @@ def rank_program(g, core, T, topo):
     fill(CF(24, 40), 4096.0)
     fill(("big", PAD + 3968, 4096), 0.0)
     op("a", lambda: g.scalar.activation(T.big[:, 0:PAD], T.cf[:, 24:40], F.Silu), [CF(24, 40)], [("big", 0, PAD)])
-    for d in (3, 2, 1):
-        ts(YI(33 + d), YI(0), d, A.logical_shift_right, 1, A.bitwise_and)
-    cp(CF(3), YI(36))
-    ts(CF(2), YI(36), -1.0, A.mult, 1.0, A.add)
-    ts(BIAS, YI(34, 37), 2 * BIG, A.mult, -BIG, A.add)
+    for d in range(4):
+        ts(YI(2 + d), YI(0), d, A.logical_shift_right, 1, A.bitwise_and)
+    ts(YI(6), YI(0), 3, A.bitwise_and)
+    ts(YI(7), YI(0), 4, A.logical_shift_right)
+    ts(YI(8, 10), YI(0, 2), 15, A.bitwise_and)
+    cp(CF(50, 60), YI(0, 10))
+    BIT, LOW2, GRP, LOW4, PART = [CF(52 + d) for d in range(4)], CF(56), CF(57), CF(58), CF(50)
+    ts(CF(2), BIT[3], -1.0, A.mult, 1.0, A.add)
+
+    def lin(out, a, k, c):
+        op("a", lambda: g.scalar.activation(ap(out), ap(a), F.Identity, bias=val(c), scale=val(k)),
+           [a] + [x for x in (k, c) if isinstance(x, tuple)], [out])
+
+    hops = first_hops(core, T, topo)
+    ring = peers(core, T, topo)
+    owners = [T.rank_of(c) for c in ring[::-1]]
+    lin(CF(4), BIT[1], -BIG, 2048.0)
+    lin(BIAS, CF(53, 56), 2 * BIG, -BIG)
+    lin(CF(5), BIT[2], -BIG, CF(4))
+    lin(CF(22), BIT[0], 63.0, 1.0)
+    lin(OFS, BIT[3], -BIG, CF(5))
+    lin(CF(23), BIT[1], 9.0 * 4095, 9.0)
+    lin(CF(47), BIT[3], 4.0, LOW2)
+    lin(CF(40), LOW2, -1.0, 3.0)
+    lin(CF(41), CF(22), CF(23), 0.0)
+    lin(CF(44), LOW2, 8.0, GRP)
+    lin(CF(48), LOW4, -1.0, 16.0)
+    lin(CF(6), BIT[2], 16.0, CF(47))
+    for h in range(2):
+        lin(CF(7 + h), BIT[2], 16.0 * (owners[2 * h + 1] - owners[2 * h]), CF(47))
     for c in range(OPT["junk"]):
         act(("big", 4096 + 256 * c, 4352 + 256 * c), ("ym", 0, 256))
-    for i, (by, col) in enumerate(((0.0, 3), (-8.0, 3), (0.0, 2), (8.0, 2))):
-        ts(("wx", 128 * ((i + 2) % 4), 128 * ((i + 2) % 4) + 128), (XI, 0, 128), by, A.is_equal, CF(col), A.mult)
-    op("v", lambda: V.tensor_reduce(ap(CF(21)), ap(BIAS), AxisListType.X, A.add), [BIAS], [CF(21)])
+    for i, (by, col) in enumerate(((0.0, BIT[3]), (-8.0, BIT[3]), (0.0, CF(2)), (8.0, CF(2)))):
+        ts(("wx", 128 * ((i + 2) % 4), 128 * ((i + 2) % 4) + 128), (XI, 0, 128), by, A.is_equal, col, A.mult)
 
     def sel(s):
         ts(("ws", 128 * s, 128 * s + 128), ("ym", 128 * (s // 8), 128 * (s // 8) + 128), float(s), A.is_equal)
@@ -319,15 +347,11 @@ def rank_program(g, core, T, topo):
         sel(s)
     ts(("lh", 0, 128), ("li", 0, 128), 2048.0, A.subtract)
     ts(("lh", 128, 256), ("ri", 0, 128), 2048.0, A.subtract)
-    ts(OFS, CF(21), -0.5, A.mult, 2048.0 - 1.5 * BIG, A.add)
     for s in range(OPT["late"], 16):
         sel(s)
 
-    hops = first_hops(core, T, topo)
-    ring = peers(core, T, topo)
     dests = ring[:-1]
-    masks = {d: bits(es) for d, es in engine_sets(core, T, topo).items()}
-    sent = sum(len(es) for es in engine_sets(core, T, topo).values())
+    sent = sum(len(es) for apart in (False, True) for es in engine_sets(core, T, topo, apart).values())
     come = {True: 0, False: 0}
     for c in dests:
         last = first_hops(c, T, topo)[core]
@@ -335,6 +359,7 @@ def rank_program(g, core, T, topo):
 
     def send(ds, src, dst, sem):
         order("g", [src(d) for d in ds], [])
+        masks = {d: bits(es) for d, es in engine_sets(core, T, topo, len(ds) < len(dests)).items()}
         trs = []
         for d in ds:
             rid, pid = topo.addr(hops[d], core)
@@ -343,92 +368,62 @@ def rank_program(g, core, T, topo):
                                          src=ap(src(d)), dst=ap(o)))
         g.remote_dma_fused(trs, local_sem=T.sem.snt)
 
-    owners = [T.rank_of(c) for c in ring[::-1]]
     iota(YI(40, 44), [[32, 2], [8, 2]], 0, 0)
     for h in range(2):
         iota(YI(44 + 2 * h, 46 + 2 * h), [[8, 2]], 16 * owners[2 * h], 0)
     iota(("low", 0, 128), [[0, 2], [-1, 64]], 128, 0)
-    send(dests, lambda d: ("cl", 16 * T.rank_of(d), 16 * T.rank_of(d) + 16),
-         lambda d: ("qv", asks_at(core, d, T, topo), asks_at(core, d, T, topo) + 16), T.sem.rq)
-    note(("rq", come[True] + come[False]), [], [("qv", 0, 48)])
     for c in range(4):
-        iota(("pay", 1024 * c, 1024 * c + 1024), [[-16, 4], [-1, 4], [0, 64]], 126 - 4 * c, 0)
+        if c == OPT["pre"]:
+            send(dests, lambda d: ("cl", 16 * T.rank_of(d), 16 * T.rank_of(d) + 16),
+                 lambda d: ("qv", asks_at(core, d, T, topo), asks_at(core, d, T, topo) + 16), T.sem.rq)
+            note(("rq", come[True] + come[False]), [], [("qv", 0, 48)])
+        iota(("pay", 1024 * c, 1024 * c + 1024), [[-8, 4], [-1, 4], [0, 64]], 126 - 32 * (c // 2) - 4 * (c % 2), 0)
         if c % 2:
             o = ("pay", 1024 * c - 1024, 1024 * c + 1024)
             order("s", [("low", 0, 128)], [o])
             g.sync.dma_start(T.pay[1:128:16, o[1]:o[2]], T.low[:, 0:128]).then_inc(T.sem["dp%d" % (c // 2)], 16)
             note(("dp%d" % (c // 2), 16), [("low", 0, 128)], [o])
-    iota(("big", 4096 + 256 * OPT["junk"], 8192), [[0, 4096 - 256 * OPT["junk"]]], M21, 0)
-    iota(("kc", 0, 128), [[1, 8], [0, 16]], 0, 0)
+    c = 4096 + 256 * OPT["junk"] + OPT["vj"]
+    iota(("big", c, 8192), [[0, 8192 - c]], M21, 0)
+    for h in range(2):
+        iota(("kc", 64 * h, 64 * h + 64), [[2 * (owners[2 * h + 1] - owners[2 * h]), 2], [1, 2], [0, 16]], 2 * owners[2 * h], 0)
 
     QV = ("qp", 0, 128)
 
     def setup():
-        ts(YI(37), YI(0), 3, A.bitwise_and)
-        yield
-        ts(YI(33), YI(0), 1, A.bitwise_and)
-        yield
-        ts(YI(16, 18), YI(0, 2), 15, A.bitwise_and)
-        yield
-        ts(YI(32), YI(0), 4, A.logical_shift_right)
-        yield
-        ts(OH, YI(16, 18), 0.0, A.is_equal)
-        yield
-        cp(GRP, YI(32))
-        yield
-        ts(CF(22), YI(33), 63.0, A.mult, 1.0, A.add)
-        yield
-        ts(CF(23), YI(34), 9.0 * 4095, A.mult, 9.0, A.add)
-        yield
-        cp(CF(46), YI(37))
-        yield
-        ts(CF(40), YI(37), -1.0, A.mult, 3.0, A.add)
-        yield
-        tt(CF(41), CF(22), CF(23), A.mult)
-        yield
-        ts(CF(47), YI(36), 4.0, A.mult, CF(46), A.add)
+        ts(OH, CF(58, 60), 0.0, A.is_equal)
         yield
         ts(("wp", 0, 136), ("xi", 0, 136), CF(40), A.is_equal, CF(41), A.mult)
         yield
-        ts(CF(24), YI(35), 16.0, A.mult, CF(47), A.add)
+        ts(("pl", 0, 4), YI(40, 44), CF(6), A.add)
         yield
         for h in range(2):
-            ts(CF(25 + h), YI(35), 16.0 * (owners[2 * h + 1] - owners[2 * h]), A.mult, CF(47), A.add)
-            yield
-        ts(CF(44), YI(37), 8.0, A.mult, GRP, A.add)
-        yield
-        ts(("pl", 0, 4), YI(40, 44), CF(24), A.add)
-        yield
-        for h in range(2):
-            ts(("pl", 4 + 2 * h, 6 + 2 * h), YI(44 + 2 * h, 46 + 2 * h), CF(25 + h), A.add)
+            ts(("pl", 4 + 2 * h, 6 + 2 * h), YI(44 + 2 * h, 46 + 2 * h), CF(7 + h), A.add)
             yield
         ts(("bm", 0, 144), ("xi", 0, 144), 16.0, A.is_equal, CF(0), A.mult)
+        lin(CF(49), CF(0), 64.0, CF(1))
         yield
-
-    def setup2():
         ts(("wi", 0, 128), ("xi", 0, 128), 0.0, A.is_equal)
         yield
+        ts(("gm", 0, 32), ("xi", 0, 32), PART, A.add, CF(44), A.is_equal)
+        yield
+        ts(("bh", 0, 144), ("xi", 0, 144), CF(48), A.is_equal, CF(49), A.mult)
+        yield
+        if OPT["pid"]:
+            ts(("we", 0, 128), ("xi", 0, 128), 0.0, A.is_equal)
+            yield
+
+    def setup2():
         for d in range(1, 6):
-            ts(("sb", 128 * d - 128, 128 * d), QV, float(S[d]), A.is_ge, 2.0 ** -d, A.mult)
+            ts(("sb", 128 * d - 128, 128 * d), ("qo", 0, 128), float(S[d] - S[1] + PAD), A.is_ge, 2.0 ** -d, A.mult)
             yield
         mm(PS(7, 0, 128), [(("wi", 0, 128), ("sb", 128 * d, 128 * d + 128)) for d in range(5)])
-        ts(("bt", 0, 144), ("xi", 0, 144), 15.0, A.is_equal, CF(1), A.mult)
-        yield
-        ts(("bh", 0, 144), ("bm", 0, 144), 64.0, A.mult)
-        yield
         tt(("qi", 0, 128), PS(6, 0, 128), QV, A.min)
-        yield
-        tt(("bh", 0, 144), ("bh", 0, 144), ("bt", 0, 144), A.add)
         yield
         ts(("m2", 0, 128), PS(7, 0, 128), -1.0, A.add)
         yield
         cp(("qo", 128, 256), ("qi", 0, 128))
         yield
-
-    def setup3():
-        cp(CF(45), YI(0))
-        ts(("kc", 0, 128), ("kc", 0, 128), 0.125, A.mult)
-        ts(("gm", 0, 32), ("xi", 0, 32), CF(45), A.add, CF(44), A.is_equal)
 
     early, more = setup(), setup2()
 
@@ -459,20 +454,26 @@ def rank_program(g, core, T, topo):
             if s % 2:
                 run(some(2))
 
-    for d, cuts, k in ((2, (0, 128, 384, 704, 1024), 4), (3, (0, 128, 320, 512), 4), (4, (0, 96, 256), 3)):
+    for d, cuts, k in OPT["cuts"]:
         win = ("big", 0, G(d, 0, 0)[1])
-        run(some(k))
         for a, m in [(x, y - x) for x, y in zip(cuts, cuts[1:])]:
             t, col = ("xa", a, a + m), CF(15 + d)
-            op("a", lambda: g.scalar.activation(ap(t), ap(win).indirect(ap(OFF(d, 1, a, a + m))), F.Identity, bias=ap(col)),
-               [win, OFF(d, 1, a, a + m), col], [t])
+            if a or not OPT["own"]:
+                op("a", lambda: g.scalar.activation(ap(t), ap(win).indirect(ap(OFF(d, 1, a, a + m))), F.Identity, bias=ap(col)),
+                   [win, OFF(d, 1, a, a + m), col], [t])
+            else:
+                op("v", lambda: V.tensor_scalar(ap(t), ap(win).indirect(ap(OFF(d, 1, a, a + m))), ap(col), None, A.add),
+                   [win, OFF(d, 1, a, a + m), col], [t])
+            if not a:
+                run(some(k))
             op("v", lambda: V.tensor_tensor(ap(G(d, a, a + m)), ap(win).indirect(ap(OFF(d, 0, a, a + m))), ap(t), A.max),
                [win, OFF(d, 0, a, a + m), t], [G(d, a, a + m)])
     win = ("big", 0, G(5, 0, 0)[1])
-    run(early)
     for side in (0, 1):
         gather("v", ("pi", side, 256, 2), win, OFF(5, side, 0, 128))
     gather("a", G(5, 0, 128), win, OFF(5, 0, 0, 128))
+    run(early)
+    W1, W2, WW = OPT["wide"]
 
     LF = ("lf", 0, 4096)
 
@@ -482,7 +483,7 @@ def rank_program(g, core, T, topo):
 
     def words(c):
         for side in (0, 1):
-            mm(PS(c, 128 * side, 128 * side + 128),
+            mm(PS(c // 2, 256 * side + 128 * (c % 2), 256 * side + 128 * (c % 2) + 128) if W1 else PS(c, 128 * side, 128 * side + 128),
                [(("wp", 3 - k, 131 - k), ("c1", 1024 * c + 256 * k + side, 1024 * c + 256 * k + 256, 2)) for k in range(4)])
 
     def empty_bits(a, b):
@@ -505,35 +506,42 @@ def rank_program(g, core, T, topo):
             yield
 
     def up(d, lo, hi, i):
-        a, b = ("ta", 256 * i, 256 * i + hi - lo), ("tb", 256 * i, 256 * i + hi - lo)
+        a, b = ("ta", 512 * i, 512 * i + hi - lo), ("tb", 512 * i, 512 * i + hi - lo)
         tt(a, H(d - 1, 0, lo, hi), H(d - 1, 1, lo, hi), A.add)
         yield
         outs = [H(d, s, lo // 2, hi // 2) for s in (0, 1)] if d < 5 else [H(d, 0, lo, hi)]
         yield from fitch(a, b, outs, PS(4 + i, 0, hi - lo) if hi - lo > 32 else None)
 
-    def level1(c, i):
-        w = ("tb", 256 * i, 256 * i + 256)
-        cp(w, PS(c, 0, 256))
+    def level1(c, i, m):
+        w = ("tb", 512 * i, 512 * i + 2 * m)
+        cp(w, PS(c, 0, 2 * m))
         yield
         for s in (0, 1):
-            ts(H(0, s, 128 * c, 128 * c + 128), sub(w, 128 * s, 128 * s + 128), M21, A.bitwise_and)
+            ts(H(0, s, m * c, m * c + m), sub(w, m * s, m * s + m), M21, A.bitwise_and)
             yield
-        yield from up(1, 128 * c, 128 * c + 128, i)
+        yield from up(1, m * c, m * c + m, i)
 
-    def table(cls, d):
-        src, sem = (("uf", "us", "af")[cls], B[d], B[d + 1]), "t%d%d" % (cls, d)
-        out = ("big", 4 * B[d], 4 * B[d + 1], 1, cls)
-        order("s", [src], [out])
-        g.sync.dma_start(T.big[cls:128:4, out[1]:out[2]], ap(src)).then_inc(T.sem[sem], 16)
-        note((sem, 16), [src], [out])
+    def table(cls, levels, halves=(0, 1)):
+        srcs = [(("uf", "us", "af")[cls], B[d] + h * (512 >> d), B[d] + (h + 1) * (512 >> d)) for d in levels for h in halves]
+        outs = [("big", 4 * x[1], 4 * x[2], 1, cls) for x in srcs]
+        sem = "t%d%d%d" % (cls, levels[0], halves[0])
+        order("s", srcs, outs)
+        for src, out in zip(srcs, outs):
+            g.sync.dma_start(T.big[cls:128:4, out[1]:out[2]], ap(src)).then_inc(T.sem[sem], 16)
+        note((sem, 16 * len(srcs)), srcs, outs)
 
-    def level_out(d, cls=0):
-        if d < 5:
-            for s in (0, 1):
-                widen((("uf", "us")[cls], B[d] + s, B[d + 1], 2), H(d, s ^ cls, 0, 512 >> d))
-        else:
-            widen(("uf", B[d], B[d + 1]), H(d, 0, 0, 32))
-        table(cls, d)
+    def words_out(cls, a, b):
+        for s in (0, 1):
+            widen((("uf", "us")[cls], a + s, b, 2), ("u", 1024 * (s ^ cls) + a // 2, 1024 * (s ^ cls) + b // 2))
+
+    LC = (0,) if OPT["sg"] else (0, 1)
+
+    def half_out(d, h):
+        for cls in (0, 1) if d else LC:
+            words_out(cls, B[d] + h * (512 >> d), B[d] + (h + 1) * (512 >> d))
+            if d and not h:
+                table(cls, (d,), (h,))
+        yield
 
     def to_list(out, src, wt="bm"):
         w = src[2] - src[1]
@@ -565,21 +573,31 @@ def rank_program(g, core, T, topo):
         spread("a", OPT["llc"], 4096)
         yield
 
-    def now(k):
-        return late(OPT["a0"][1], clades()) if OPT["a0"][0] == k else ()
+    def first_half():
+        yield from late(3, half_out(0, 0))
+        yield from late(6, half_out(1, 0))
 
-    run(level1(0, 0), late(2, level1(1, 1)), iter(now(0)))
-    run(level1(2, 0), late(2, level1(3, 1)), iter(now(1)))
-    level_out(0)
-    level_out(0, 1)
-    level_out(1)
-    run(up(2, 0, 128, 0), late(2, up(2, 128, 256, 1)), iter(now(2)))
-    level_out(1, 1)
-    level_out(2)
-    run(up(3, 0, 64, 0), late(2, up(3, 64, 128, 1)))
-    level_out(3)
-    run(up(4, 0, 64, 0), some(8, more))
-    level_out(4)
+    run(level1(0, 0, 256), late(OPT["l1"], level1(1, 1, 256)), late(OPT["a0"], clades()), first_half(),
+        late(OPT["l1"] + 3, half_out(0, 1)))
+    run(half_out(1, 1))
+    for h in range(2):
+        for cls in LC:
+            table(cls, (0,), (h,))
+    for cls in (0, 1):
+        table(cls, (1,), (1,))
+    if W2:
+        run(up(2, 0, 256, 0), late(1, some(5, more)))
+        run(up(3, 0, 128, 0))
+    else:
+        run(up(2, 0, 128, 0), late(2, up(2, 128, 256, 1)))
+        run(up(3, 0, 128, 0), late(1, some(5, more)))
+    for cls in (0, 1):
+        words_out(cls, B[2], B[4])
+        table(cls, (2, 3))
+    run(up(4, 0, 64, 0), late(2, some(3, more)))
+    for cls in (0, 1):
+        words_out(cls, B[4], B[5])
+        table(cls, (4,))
 
     def sums(d, out, par, lo, hi):
         for s in (0, 1):
@@ -588,42 +606,40 @@ def rank_program(g, core, T, topo):
 
     def down3():
         for s in (0, 1):
-            cp(("o", s, 64, 2), H(4, 1 - s, 0, 32))
+            cp(("o", 128 + s, 192, 2), H(4, 1 - s, 0, 32))
             yield
-        yield from sums(3, ("ai", 256, 384), ("o", 0, 64), 0, 64)
-        yield from fitch(("ai", 256, 384), ("tb", 256, 384), [("o", 64, 192)], PS(5, 0, 128))
+        yield from sums(3, ("ai", 256, 384), ("o", 128, 192), 0, 64)
+        yield from fitch(("ai", 256, 384), ("tb", 512, 640), [("o", 0, 128)], PS(5, 0, 128))
 
-    def down2(i):
-        yield from sums(2, ("ai", 0, 256), ("o", 64, 192), 64 * i, 64 * i + 64)
-        yield from fitch(("ai", 128 * i, 128 * i + 128), ("tb", 256 * i, 256 * i + 128), [("o", 192 + 128 * i, 320 + 128 * i)],
-                         PS(4 + i, 0, 128))
+    def down2(i, m):
+        yield from sums(2, ("ai", 0, 256), ("o", 0, 128), m // 2 * i, m // 2 * (i + 1))
+        yield from fitch(("ai", m * i, m * i + m), ("tb", 512 * i, 512 * i + m), [("o", 192 + m * i, 192 + m * i + m)],
+                         PS(4 + i, 0, m))
         for s in (0, 1):
-            cp(("af", B[1] + 256 * i + s, B[1] + 256 * i + 256, 2), ("o", 192 + 128 * i, 320 + 128 * i))
+            cp(("af", B[1] + 2 * m * i + s, B[1] + 2 * m * (i + 1), 2), ("o", 192 + m * i, 192 + m * i + m))
+            if s:
+                table(2, (1,), (i,) if m == 128 else (0, 1))
             yield
 
-    def outside(d, src):
-        for s in (0, 1):
-            widen(("af", B[d] + s, B[d + 1], 2), src)
-        table(2, d)
 
-    def lookup(e, h):
-        x = ("xh", 1024 * h, 1024 * h + 1024)
-        gather(e, x, POS, QO(2 + h))
-        to_list(PS(7 - h, 0, 64), x, "bh")
+    def lookup(e, h, a, b):
+        gather(e, ("xh", 1024 * h + a, 1024 * h + b), POS, QO(2 + h, a // 16, b // 16))
 
-    def index(h):
-        p = PS(7 - h, 0, 64)
-        t = QI(3 + h)
-        tt(t, p, ("m2", 64 * h, 64 * h + 64), A.mult)
-        yield
-        if not h:
-            ts(QO(4), t, 8192.0, A.add)
-            answer()
-            yield
-            return
-        ts(QO(6), t, 0.5, A.mult, 4095.75, A.add)
-        ts(QO(5), t, 8192.0, A.add)
-        yield
+    def listed(h, a=0, b=64):
+        to_list(PS(7 - h - 3 * (a > 0), a, b), ("xh", 1024 * h + 16 * a, 1024 * h + 16 * b), "bh")
+
+    def index(h, a=0, b=64):
+        t = QI(3 + h, a, b)
+        tt(t, PS(7 - h - 3 * (a > 0), a, b), ("m2", 64 * h + a, 64 * h + b), A.mult)
+        if h:
+            ts(QO(6, a, b), t, 0.5, A.mult, 4095.75, A.add)
+        ts(QO(4 + h, a, b), t, 8192.0, A.add)
+
+    def sibling():
+        ts(QI(5), QO(6), 4.0, A.mult, -8191.0, A.add)
+        tt(QI(5), QI(5), QI(4), A.subtract)
+        tt(QI(5), QI(5), QI(7), A.max)
+        cp(QO(7), QI(5))
 
     TAB = ("big", 0, 8192)
 
@@ -634,81 +650,113 @@ def rank_program(g, core, T, topo):
 
     def operand(e, i, h):
         x = ("xv", 1024 * (i + 1) + 512 * h, 1024 * (i + 1) + 512 * h + 512)
+        if (i, h) in OPT["pe"]:
+            for k in range(4):
+                y = sub(x, 128 * k, 128 * k + 128)
+                gather(e, y, ("big", 4096, 8192), QO(6, 32 * h + 8 * k, 32 * h + 8 * k + 8))
+                op("p", lambda: g.tensor.matmul(ap(PS(1 + h, 0, 128)), T.we[:, 131 - k:259 - k], ap(y), k == 0, k == 3),
+                   [y, ("we", 128, 264)], [PS(1 + h, 0, 128)])
+            return
+        if OPT["sg"] and i:
+            gather(e, x, TAB, QO(3 + 2 * i, 32 * h, 32 * h + 32))
+            c = 256 * (4 - i) + 128 * h
+            moved("s", "d%d" % (8 - 2 * i + h), 0, ("so", c, c + 128), x)
+            return
         gather(e, x, TAB if i else ("big", 4096, 8192), QO(6 - i, 32 * h, 32 * h + 32))
         for j, cls in enumerate((1, 0) if i else (2, 1)):
             c = 256 * (2 * i + j) + 128 * h
             moved("s", "d%d" % (4 * i + 2 * j + h), cls, ("so", c, c + 128), x)
 
-    def answer():
-        for h in range(2):
-            x, out = ("xv", 512 * h, 512 * h + 512), ("land", 128 * h, 128 * h + 128)
-            gather("a", x, TAB, QO(4, 32 * h, 32 * h + 32))
-            moved("s", "dc%d" % h, 0, out, x)
-        for ds in ([d for d in dests if hops[d] != d], [d for d in dests if hops[d] == d]):
-            send(ds, lambda d: ("land", 64 * ring.index(d), 64 * ring.index(d) + 64),
-                 lambda d: ("land", lands_at(core, d, T, topo), lands_at(core, d, T, topo) + 64), T.sem.rp)
-        note(("rp", come[True]), [], [("land", 256, 320)])
-        note(("rp2", come[False]), [], [("land", 320, 448)])
+    def answer(e, h):
+        x, out = ("xv", 512 * h, 512 * h + 512), ("land", 128 * h, 128 * h + 128)
+        if h == 0 and OPT["pc"]:
+            for k in range(4):
+                y = sub(x, 128 * k, 128 * k + 128)
+                gather(e, y, TAB, QO(4, 8 * k, 8 * k + 8))
+                op("p", lambda: g.tensor.matmul(ap(PS(0, 0, 128)), T.we[:, 267 - k:395 - k], ap(y), k == 0, k == 3),
+                   [y, ("we", 264, 400)], [PS(0, 0, 128)])
+            return
+        gather(e, x, TAB, QO(4, 32 * h, 32 * h + 32))
+        moved("s", "dc%d" % h, 0, out, x)
+        reply(h)
+
+    def out_of_psum(e):
+        (act if e == "a" else cp)(("land", 0, 128), PS(0, 0, 128))
+        reply(0)
+
+    def reply(h):
+        send([d for d in dests if (hops[d] == d) == bool(h)], lambda d: ("land", 64 * ring.index(d), 64 * ring.index(d) + 64),
+             lambda d: ("land", lands_at(core, d, T, topo), lands_at(core, d, T, topo) + 64), T.sem.rp)
+
+    note(("rp", come[True]), [], [("land", 256, 320)])
+    note(("rp2", come[False]), [], [("land", 320, 448)])
 
     run(up(5, 0, 32, 0), down3(), late(2, more))
-    level_out(5)
-    for e, h in OPT["le"]:
-        if e == "a":
-            lookup(e, h)
-    outside(2, ("o", 64, 192))
-    outside(3, ("o", 0, 64))
-    for d in (2, 3, 4):
-        level_out(d, 1)
-    run(down2(0), late(2, down2(1)))
-    table(2, 1)
-    setup3()
-    for e, h in OPT["le"]:
-        if e == "v":
-            lookup(e, h)
-    for h in OPT["ix"]:
-        run(index(h))
-    for e, i, h in OPT["ops"]:
-        operand(e, i, h)
+    widen(("uf", B[5], B[6]), H(5, 0, 0, 32))
+    table(0, (5,))
+    for s in (0, 1):
+        widen(("af", B[2] + s, B[4], 2), ("o", 0, 192))
+    table(2, (2, 3))
+    steps = {"L": lookup, "T": listed, "I": index, "O": operand, "A": answer, "R": out_of_psum, "S": sibling}
 
-    def walk(h):
-        lo, hi = 128 * h, 128 * h + 128
+    def take(sts):
+        for st in sts:
+            steps[st[0]](*st[1:])
+        yield
+
+    if W2:
+        run(down2(0, 256), late(OPT["ic"], take(OPT["mid"])))
+    else:
+        run(down2(0, 128), late(2, down2(1, 128)), late(OPT["ic"], take(OPT["mid"])))
+    run(take(OPT["tail"]))
+    lin(("kc", 0, 128), ("kc", 0, 128), 0.125, 0.0)
+
+    def low(e, fn, reads, writes):
+        op(e, lambda: fn(*[T[r[0]][0:64, r[1]:r[2]] for r in writes + reads]), reads, writes)
+
+    def walk(h, m):
+        lo, hi = m * h, m * h + m
         a, b, x = ("ta", lo, hi), ("tb", lo, hi), ("o", lo, hi)
-        spare = PS(1 + h, 128, 256)
+        spare = PS(1 + h, 0, m)
         for i in (1, 2, 3):
-            tt(a, x if i > 1 else ("so", lo, hi), ("so", 256 * i + lo, 256 * i + hi), A.add)
+            y = ("so", 256 * i + lo, 256 * i + hi)
+            if i == 1 and OPT["pid"]:
+                for j in (2, 3):
+                    mm(PS(3 + h, m * j - 2 * m, m * j - m), [(("we", 0, 128), ("so", 256 * j + lo, 256 * j + hi))])
+            if i > 1 and OPT["pid"]:
+                y = PS(3 + h, m * i - 2 * m, m * i - m)
+            tt(a, x if i > 1 else ("so", lo, hi), y, A.add)
             yield
             yield from fitch(a, b, [x], spare)
         tt(a, x, ("land", 192 + lo, 192 + hi), A.add)
         yield
         yield from empty_bits(a, b)
         cp(("nzf", lo, hi), b)
-        for j in (2 * h, 2 * h + 1):
-            q = owners[j]
-            op("p", lambda: g.tensor.matmul(T.ps7[0:64, 32 * q:32 * q + 32], T.nzf[:, 64 * j:64 * j + 64], T.gm[:, 0:32], True, True),
-               [("nzf", 64 * j, 64 * j + 64), ("gm", 0, 32)], [PS(7, 32 * q, 32 * q + 32)])
+        for j in range(lo // 64, hi // 64):
+            o, y = PS(7, 32 * j, 32 * j + 32), ("nzf", 64 * j, 64 * j + 64)
+            op("p", lambda: g.tensor.matmul(T[o[0]][0:64, o[1]:o[2]], ap(y), T.gm[:, 0:32], True, True), [y, ("gm", 0, 32)], [o])
         yield
 
-    run(walk(0), late(OPT["lag"], walk(1)))
-
-    op("v", lambda: V.tensor_scalar(T.ki[0:64, :], T.ps7[0:64, 0:128], ONES / 262144.0, None, A.mult), [PS(7, 0, 128)], [("ki", 0, 128)])
-    op("v", lambda: V.tensor_scalar(T.ki[0:64, :], T.ki[0:64, :], 63, None, A.bitwise_and), [("ki", 0, 128)], [("ki", 0, 128)])
-    op("v", lambda: V.tensor_tensor(T.kf[0:64, 0:128], T.ki[0:64, :], T.kc[0:64, :], A.add),
-       [("ki", 0, 128), ("kc", 0, 128)], [("kf", 0, 128)])
-    a = 0
-    for w in (64, 32, 16):
-        out = T.kf[0:64, a + 2 * w:a + 3 * w] if w > 16 else T.kb[0:64, :]
-        op("v", lambda: V.tensor_tensor(out, T.kf[0:64, a:a + w], T.kf[0:64, a + w:a + 2 * w], A.min),
-           [("kf", a, a + 2 * w)], [("kf", a + 2 * w, a + 3 * w), ("kb", 0, 16)])
-        a += 2 * w
+    if WW:
+        run(walk(0, 256))
+    else:
+        run(walk(0, 128), late(OPT["lag"], walk(1, 128)))
+    k, f = ("ki", 0, 128), ("kf", 0, 128)
+    low("v", lambda o, y: V.tensor_scalar(o, y, ONES / 262144.0, None, A.mult), [PS(7, 0, 128)], [k])
+    low("v", lambda o, y: V.tensor_scalar(o, y, 63, None, A.bitwise_and), [k], [k])
+    low("v", lambda o, y, z: V.tensor_tensor(o, y, z, A.add), [k, ("kc", 0, 128)], [f])
+    low("v", lambda o, y, z: V.tensor_tensor(o, y, z, A.min), [sub(f, 0, 64), sub(f, 64, 128)], [("kf", 128, 192)])
+    low("v", lambda o, y, z: V.tensor_tensor(o, y, z, A.min), [("kf", 128, 160), ("kf", 160, 192)], [("kf", 192, 224)])
+    low("v", lambda o, y, z: V.tensor_tensor(o, y, z, A.min), [("kf", 192, 208), ("kf", 208, 224)], [("kb", 0, 16)])
     for h in range(2):
-        op("p", lambda: g.tensor.matmul(T.ps0[0:8, 64 * h:64 * h + 64], T.kb[0:64, 8 * h:8 * h + 8], T.wi[0:64, 0:64], True, True),
-           [("kb", 0, 16), ("wi", 0, 64)], [PS(0, 64 * h, 64 * h + 64)])
-    op("v", lambda: V.tensor_scalar(T.ei[0:8, :], T.ps0[0:8, 0:128], -0.4375, None, A.add), [PS(0, 0, 128)], [("ei", 0, 128)])
+        op("p", lambda: g.tensor.matmul(T.ps5[0:8, 64 * h:64 * h + 64], T.kb[0:64, 8 * h:8 * h + 8], T.wi[0:64, 0:64], True, True),
+           [("kb", 0, 16), ("wi", 0, 64)], [PS(5, 64 * h, 64 * h + 64)])
+    op("v", lambda: V.tensor_scalar(T.ei[0:8, :], T.ps5[0:8, 0:128], -0.4375, None, A.add), [PS(5, 0, 128)], [("ei", 0, 128)])
     op("v", lambda: V.tensor_copy(T.ef[0:8, 0:128], T.ei[0:8, :]), [("ei", 0, 128)], [("ef", 0, 128)])
     order("s", [("ef", 0, 128)], [])
     g.sync.dma_start(T.cost[:], T.ef[0:8, 0:128]).then_inc(T.sem.do1, 16)
-    op("v", lambda: V.tensor_tensor(T.ef[0:8, 256:384], T.ps0[0:8, 0:128], T.ei[0:8, :], A.subtract),
-       [PS(0, 0, 128), ("ei", 0, 128)], [("ef", 256, 384)])
+    op("v", lambda: V.tensor_tensor(T.ef[0:8, 256:384], T.ps5[0:8, 0:128], T.ei[0:8, :], A.subtract),
+       [PS(5, 0, 128), ("ei", 0, 128)], [("ef", 256, 384)])
     op("v", lambda: V.tensor_scalar(T.ef[0:8, 128:256], T.ef[0:8, 256:384], 8.0, None, A.mult),
        [("ef", 256, 384)], [("ef", 128, 256)])
     order("a", [("ef", 128, 256)], [])
@@ -716,6 +764,6 @@ def rank_program(g, core, T, topo):
 
     for e in cnt:
         wait("g", (e, cnt[e]))
-    wait("g", ("snt", 2 * sent))
+    wait("g", ("snt", sent))
     wait("g", ("do1", 16))
     wait("g", ("do2", 16))

from concourse.bass import DstId, RemoteDMATransfer
from concourse.mybir import AluOpType, ActivationFunctionType, AxisListType

S = [0, 4096, 6144, 7168, 7680, 7936, 8064]
ONES = 1 + 64 + 4096 + 262144
M21 = 21 * ONES
PB = 64
PAD = 16
BIG = 8192.0
B = [2048 - (2048 >> d) for d in range(7)]

SCRATCH = {
    "lf": ("sbuf", [128, 4096], "bfloat16"),
    "c1": ("sbuf", [128, 4096], "bfloat16"),
    "li": ("sbuf", [128, 248], "int32"),
    "ri": ("sbuf", [128, 248], "int32"),
    "cl": ("sbuf", [128, 64], "int32"),
    "qv": ("sbuf", [128, 128], "int32"),
    "lh": ("sbuf", [128, 256], "float16"),
    "wx": ("sbuf", [128, 512], "float16"),
    "lx": ("sbuf", [128, 256], "float16"),
    "ws": ("sbuf", [128, 2048], "float16"),
    "kb": ("sbuf", [128, 16], "bfloat16"),
    "off": ("sbuf", [128, 240], "uint16"),
    "pi": ("sbuf", [128, 256], "uint16"),
    "qo": ("sbuf", [128, 640], "uint16"),
    "qi": ("sbuf", [128, 512], "int32"),
    "big": ("sbuf", [128, 8192], "float32"),
    "pay": ("sbuf", [128, 4096], "float32"),
    "pos": ("sbuf", [128, 4096], "float32"),
    "xa": ("sbuf", [128, 2048], "float32"),
    "low": ("sbuf", [128, 320], "float32"),
    "xh": ("sbuf", [128, 2048], "bfloat16"),
    "xv": ("sbuf", [128, 5120], "float32"),
    "so": ("sbuf", [128, 1024], "float32"),
    "u": ("sbuf", [128, 2080], "int32"),
    "uf": ("sbuf", [128, 2048], "float32"),
    "us": ("sbuf", [128, 2048], "float32"),
    "af": ("sbuf", [128, 2048], "float32"),
    "ai": ("sbuf", [128, 512], "int32"),
    "o": ("sbuf", [128, 512], "int32"),
    "ta": ("sbuf", [128, 1024], "int32"),
    "tb": ("sbuf", [128, 1024], "int32"),
    "land": ("sbuf", [128, 448], "float32"),
    "qp": ("sbuf", [128, 128], "int32"),
    "pl": ("sbuf", [128, 8], "uint16"),
    "nzf": ("sbuf", [128, 256], "float32"),
    "sb": ("sbuf", [128, 640], "bfloat16"),
    "m2": ("sbuf", [128, 384], "float32"),
    "xi": ("sbuf", [128, 144], "float32"),
    "ym": ("sbuf", [128, 256], "bfloat16"),
    "yi": ("sbuf", [128, 72], "int32"),
    "cf": ("sbuf", [128, 72], "float32"),
    "wp": ("sbuf", [128, 136], "bfloat16"),
    "we": ("sbuf", [128, 400], "float32"),
    "wi": ("sbuf", [128, 128], "bfloat16"),
    "wf": ("sbuf", [128, 64], "float32"),
    "bm": ("sbuf", [128, 144], "float32"),
    "bh": ("sbuf", [128, 144], "bfloat16"),
    "bt": ("sbuf", [128, 144], "bfloat16"),
    "gm": ("sbuf", [128, 32], "float32"),
    "kc": ("sbuf", [128, 128], "float32"),
    "ki": ("sbuf", [128, 128], "int32"),
    "kf": ("sbuf", [128, 240], "float32"),
    "ei": ("sbuf", [128, 128], "int32"),
    "ef": ("sbuf", [128, 384], "float32"),
}
for _b in range(8):
    SCRATCH["ps%d" % _b] = ("psum", [128, 512], "float32")

SEMAPHORES = ["v", "a", "p", "g", "dl0", "dl1", "dli", "dri", "dcl", "ded", "drq", "do1", "do2",
              "t000", "t001", "t010", "t011", "t020", "t040", "t050", "t100", "t101", "t110", "t111", "t120", "t140",
              "t210", "t211", "t220", "d0", "d1", "d2", "d3", "d4", "d5", "d6", "d7", "dp0", "dp1", "dj", "dc0", "dc1", "rq", "rp", "rp2", "snt"]

OPT = {"lv": (512, 512, 512, 256), "lag": 3, "ne": 8, "llc": 768, "a0": 6, "junk": 5, "vj": 0, "pre": 1, "late": 12,
       "ev": "avavavav", "pid": 1, "mid": (), "ic": 0, "pe": (), "pc": 0, "own": 0, "sg": 0, "wide": (1, 1, 0), "l1": 4,
       "cuts": ((2, (0, 192, 576, 1024), 3), (3, (0, 160, 512), 3), (4, (0, 96, 256), 2)),
       "tail": (("L", "a", 0, 0, 1024), ("T", 0), ("L", "v", 1, 0, 512), ("L", "a", 1, 512, 1024), ("T", 1),
                ("I", 0), ("A", "a", 0), ("I", 1), ("O", "v", 0, 0), ("O", "a", 0, 1), ("O", "v", 1, 0), ("A", "a", 1),
                ("O", "a", 1, 1))}


def first_hops(src, T, topo):
    free = [c for c in topo.cores_of(src) if T.rank_of(c) is None]
    free.sort(key=lambda c: topo.die(c) != topo.die(src))
    hops = {}
    for d in T.cores:
        if d == src:
            continue
        if topo.may_write(src, d):
            hops[d] = d
        else:
            r = [c for c in free if topo.may_write(c, d)][0]
            free.remove(r)
            hops[d] = r
    return hops


def bits(engs):
    return sum(1 << e for e in engs)


def engine_sets(src, T, topo, apart=False):
    hops = first_hops(src, T, topo)
    far = [d for d in hops if hops[d] == d]
    near = [d for d in hops if hops[d] != d]
    out = topo.engines(src, far[0])
    rest = [e for e in topo.engines(src, hops[near[0]]) if apart or e not in out]
    sets = {}
    for ds, es in ((far, out), (near, rest)):
        k = len(es) // len(ds)
        for i, d in enumerate(ds):
            sets[d] = es[k * i:k * i + k][:OPT["ne"]]
    return sets


def peers(c, T, topo):
    hops = first_hops(c, T, topo)
    return sorted(hops, key=lambda d: hops[d] == d) + [c]


def asks_at(src, dst, T, topo):
    return 16 * peers(dst, T, topo).index(src)


def lands_at(src, dst, T, topo):
    return 64 * (2 * len(T.cores) - 2 - peers(dst, T, topo).index(src))


def relay_program(g, core, T, topo, src, dst):
    rid, pid = topo.addr(dst, core)
    es = topo.engines(core, dst)[:OPT["ne"]]
    got = len(engine_sets(src, T, topo)[dst])
    c = asks_at(src, dst, T, topo)
    g.wait_ge(T.sem.rq, got)
    g.remote_dma(T.qv[:, c:c + 16], T.qv[:, 0:16], T.sem.rq, T.sem.snt, pid, rid, bits(es))
    g.wait_ge(T.sem.rp, len(engine_sets(src, T, topo, True)[dst]))
    c = lands_at(src, dst, T, topo)
    g.remote_dma(T.land[:, c:c + 64], T.land[:, 0:64], T.sem.rp2, T.sem.snt, pid, rid, bits(es))
    g.wait_ge(T.sem.snt, 2 * len(es))


def rank_program(g, core, T, topo):
    me = T.rank_of(core)
    if me is None:
        for src in T.cores:
            for d, h in first_hops(src, T, topo).items():
                if h == core:
                    relay_program(g, core, T, topo, src, d)
        return
    n = len(T.cores)
    A, F = AluOpType, ActivationFunctionType
    Q = {"v": g.vector, "a": g.scalar, "p": g.tensor, "g": g, "s": g.sync}
    V = g.vector
    cnt = {"v": 0, "a": 0, "p": 0, "g": 0}
    waited = {e: {} for e in Q}
    log = {}

    def wait(e, tok):
        if waited[e].get(tok[0], 0) < tok[1]:
            Q[e].wait_ge(T.sem[tok[0]], tok[1])
            waited[e][tok[0]] = tok[1]

    def ap(r):
        return T[r[0]][:, r[1]:r[2]:r[3]] if len(r) > 3 else T[r[0]][:, r[1]:r[2]]

    def order(e, reads, writes):
        need = {}
        for r, w in [(x, False) for x in reads] + [(x, True) for x in writes]:
            for (r2, w2, tok) in log.get(r[0], []):
                if e == "p" and tok[0] == "p":
                    continue
                bank = r[0].startswith("ps") and tok[0] != e
                apart = len(r) > 3 and r[3:] == r2[3:] and (r[1] - r2[1]) % r[3] != 0
                apart = apart or (len(r) > 4 and len(r2) > 4 and r[4] != r2[4])
                if bank or ((w or w2) and r2[1] < r[2] and r[1] < r2[2] and not apart):
                    need[tok[0]] = max(need.get(tok[0], 0), tok[1])
        for k in need:
            wait(e, (k, need[k]))

    def note(tok, reads, writes):
        for r, w in [(x, False) for x in reads] + [(x, True) for x in writes]:
            log.setdefault(r[0], []).append((r, w, tok))

    def op(e, fn, reads, writes):
        order(e, reads, writes)
        ins = fn()
        cnt[e] += 1
        ins.then_inc(T.sem[e], 1)
        note((e, cnt[e]), reads, writes)

    def val(s):
        return ap(s) if isinstance(s, tuple) else s

    def ts(out, in0, s1, op0, s2=None, op1=None):
        rs = [in0] + [s for s in (s1, s2) if isinstance(s, tuple)]
        if op1 is None:
            op("v", lambda: V.tensor_scalar(ap(out), ap(in0), val(s1), None, op0), rs, [out])
        else:
            op("v", lambda: V.tensor_scalar(ap(out), ap(in0), val(s1), val(s2), op0, op1), rs, [out])

    def tt(out, a, b, o):
        op("v", lambda: V.tensor_tensor(ap(out), ap(a), ap(b), o), [a, b], [out])

    def cp(out, a):
        op("v", lambda: V.tensor_copy(ap(out), ap(a)), [a], [out])

    def fill(out, c):
        op("v", lambda: V.memset(ap(out), c), [], [out])

    def act(out, a, col=None):
        if col is None:
            op("a", lambda: g.scalar.activation(ap(out), ap(a), F.Copy), [a], [out])
        else:
            op("a", lambda: g.scalar.activation(ap(out), ap(a), F.Identity, bias=ap(col)), [a, col], [out])

    def gather(e, out, win, off):
        if e == "v":
            op("v", lambda: V.tensor_copy(ap(out), ap(win).indirect(ap(off))), [win, off], [out])
        else:
            op("a", lambda: g.scalar.activation(ap(out), ap(win).indirect(ap(off)), F.Copy), [win, off], [out])

    def scatter(e, win, off, src):
        if e == "v":
            op("v", lambda: V.tensor_copy(ap(win).indirect(ap(off)), ap(src)), [src, off], [win])
        else:
            op("a", lambda: g.scalar.activation(ap(win).indirect(ap(off)), ap(src), F.Silu), [src, off], [win])

    def mm(out, terms):
        def fn():
            for i, t in enumerate(terms):
                ins = g.tensor.matmul(ap(out), ap(t[0]), ap(t[1]), i == 0, i == len(terms) - 1)
            return ins
        op("p", fn, [r for t in terms for r in t], [out])

    def sub(r, a, b, *st):
        return (r[0], r[1] + a, r[1] + b) + st

    def iota(out, pat, base, cm):
        if out[0] == "yi":
            op("g", lambda: g.iota(ap(out), pat, base, cm), [], [out])
        else:
            op("g", lambda: g.iota(ap(out), pat, base, cm, allow_small_or_imprecise_dtypes=True), [], [out])

    def widen(out, a):
        op("g", lambda: g.affine_select(ap(out), ap(a), [[0, a[2] - a[1]]], A.is_gt, 0.0, 1, 0), [a], [out])

    def load(e, sem, out, src):
        Q[e].dma_start(ap(out), src).then_inc(T.sem[sem], 16)
        note((sem, 16), [], [out])

    def late(k, gen):
        for _ in range(k):
            yield
        yield from gen

    def run(*gens):
        gens = list(gens)
        while gens:
            for x in list(gens):
                if next(x, "end") == "end":
                    gens.remove(x)

    def PS(b, a, c):
        return ("ps%d" % b, a, c)

    def CF(a, b=None):
        return ("cf", a, a + 1 if b is None else b)

    def YI(a, b=None):
        return ("yi", a, a + 1 if b is None else b)

    def G(d, a, b):
        return ("big", PAD + S[d] - S[1] + a, PAD + S[d] - S[1] + b)

    def OFF(d, side, a, b):
        c = 120 * side + (S[d] - S[2]) // 16
        return ("off", c + a // 16, c + b // 16)

    def H(d, side, a, b):
        c = 1024 * side + B[d] // 2 if d < 5 else 2048
        return ("u", c + a, c + b)

    def QO(i, a=0, b=64):
        return ("qo", 64 * i + a, 64 * i + b)

    def QI(i, a=0, b=64):
        return ("qi", 64 * i + a, 64 * i + b)

    load("s", "dli", ("li", 0, 248), T.left[:])
    load("a", "dri", ("ri", 0, 248), T.right[:])
    load("s", "dcl", ("cl", 0, 64), T.clade[:])
    load("a", "ded", ("qv", 64, 128), T.edge[:])
    load("s", "drq", ("qv", 48, 64), T.clade[:, 16 * me:16 * me + 16])
    for j in range(2):
        load("s", "dl%d" % j, ("lf", 2048 * j, 2048 * j + 2048), T.leaf[:, 2048 * j:2048 * j + 2048])

    OH, BIAS, OFS = CF(0, 2), CF(17, 20), CF(20)
    XI = "xi"
    iota(YI(0, 2), [[-1, 2]], 0, 1)
    iota((XI, 0, 144), [[1, 144]], 0, -1)
    iota(("ym", 0, 128), [[-16, 8], [0, 8], [-8, 2]], 0, 1)
    iota(("ym", 128, 256), [[-16, 8], [0, 8], [8, 2]], 0, 1)

    fill(CF(24, 40), 4096.0)
    fill(("big", PAD + 3968, 4096), 0.0)
    op("a", lambda: g.scalar.activation(T.big[:, 0:PAD], T.cf[:, 24:40], F.Silu), [CF(24, 40)], [("big", 0, PAD)])
    for d in range(4):
        ts(YI(2 + d), YI(0), d, A.logical_shift_right, 1, A.bitwise_and)
    ts(YI(6), YI(0), 3, A.bitwise_and)
    ts(YI(7), YI(0), 4, A.logical_shift_right)
    ts(YI(8, 10), YI(0, 2), 15, A.bitwise_and)
    cp(CF(50, 60), YI(0, 10))
    BIT, LOW2, GRP, LOW4, PART = [CF(52 + d) for d in range(4)], CF(56), CF(57), CF(58), CF(50)
    ts(CF(2), BIT[3], -1.0, A.mult, 1.0, A.add)

    def lin(out, a, k, c):
        op("a", lambda: g.scalar.activation(ap(out), ap(a), F.Identity, bias=val(c), scale=val(k)),
           [a] + [x for x in (k, c) if isinstance(x, tuple)], [out])

    hops = first_hops(core, T, topo)
    ring = peers(core, T, topo)
    owners = [T.rank_of(c) for c in ring[::-1]]
    lin(CF(4), BIT[1], -BIG, 2048.0)
    lin(BIAS, CF(53, 56), 2 * BIG, -BIG)
    lin(CF(5), BIT[2], -BIG, CF(4))
    lin(CF(22), BIT[0], 63.0, 1.0)
    lin(OFS, BIT[3], -BIG, CF(5))
    lin(CF(23), BIT[1], 9.0 * 4095, 9.0)
    lin(CF(47), BIT[3], 4.0, LOW2)
    lin(CF(40), LOW2, -1.0, 3.0)
    lin(CF(41), CF(22), CF(23), 0.0)
    lin(CF(44), LOW2, 8.0, GRP)
    lin(CF(48), LOW4, -1.0, 16.0)
    lin(CF(6), BIT[2], 16.0, CF(47))
    for h in range(2):
        lin(CF(7 + h), BIT[2], 16.0 * (owners[2 * h + 1] - owners[2 * h]), CF(47))
    for c in range(OPT["junk"]):
        act(("big", 4096 + 256 * c, 4352 + 256 * c), ("ym", 0, 256))
    for i, (by, col) in enumerate(((0.0, BIT[3]), (-8.0, BIT[3]), (0.0, CF(2)), (8.0, CF(2)))):
        ts(("wx", 128 * ((i + 2) % 4), 128 * ((i + 2) % 4) + 128), (XI, 0, 128), by, A.is_equal, col, A.mult)

    def sel(s):
        ts(("ws", 128 * s, 128 * s + 128), ("ym", 128 * (s // 8), 128 * (s // 8) + 128), float(s), A.is_equal)

    for s in range(OPT["late"]):
        sel(s)
    ts(("lh", 0, 128), ("li", 0, 128), 2048.0, A.subtract)
    ts(("lh", 128, 256), ("ri", 0, 128), 2048.0, A.subtract)
    for s in range(OPT["late"], 16):
        sel(s)

    dests = ring[:-1]
    sent = sum(len(es) for apart in (False, True) for es in engine_sets(core, T, topo, apart).values())
    come = {True: 0, False: 0}
    for c in dests:
        last = first_hops(c, T, topo)[core]
        come[last == core] += len(engine_sets(c, T, topo)[core] if last == core else topo.engines(last, core)[:OPT["ne"]])

    def send(ds, src, dst, sem):
        order("g", [src(d) for d in ds], [])
        masks = {d: bits(es) for d, es in engine_sets(core, T, topo, len(ds) < len(dests)).items()}
        trs = []
        for d in ds:
            rid, pid = topo.addr(hops[d], core)
            o = dst(d) if hops[d] == d else sub(dst(d), -dst(d)[1], -dst(d)[1] + dst(d)[2] - dst(d)[1])
            trs.append(RemoteDMATransfer(dst_ids=[DstId(rid=rid, pnc=pid)], dma_engine_mask=masks[d], remote_sem=sem,
                                         src=ap(src(d)), dst=ap(o)))
        g.remote_dma_fused(trs, local_sem=T.sem.snt)

    iota(YI(40, 44), [[32, 2], [8, 2]], 0, 0)
    for h in range(2):
        iota(YI(44 + 2 * h, 46 + 2 * h), [[8, 2]], 16 * owners[2 * h], 0)
    iota(("low", 0, 128), [[0, 2], [-1, 64]], 128, 0)
    for c in range(4):
        if c == OPT["pre"]:
            send(dests, lambda d: ("cl", 16 * T.rank_of(d), 16 * T.rank_of(d) + 16),
                 lambda d: ("qv", asks_at(core, d, T, topo), asks_at(core, d, T, topo) + 16), T.sem.rq)
            note(("rq", come[True] + come[False]), [], [("qv", 0, 48)])
        iota(("pay", 1024 * c, 1024 * c + 1024), [[-8, 4], [-1, 4], [0, 64]], 126 - 32 * (c // 2) - 4 * (c % 2), 0)
        if c % 2:
            o = ("pay", 1024 * c - 1024, 1024 * c + 1024)
            order("s", [("low", 0, 128)], [o])
            g.sync.dma_start(T.pay[1:128:16, o[1]:o[2]], T.low[:, 0:128]).then_inc(T.sem["dp%d" % (c // 2)], 16)
            note(("dp%d" % (c // 2), 16), [("low", 0, 128)], [o])
    c = 4096 + 256 * OPT["junk"] + OPT["vj"]
    iota(("big", c, 8192), [[0, 8192 - c]], M21, 0)
    for h in range(2):
        iota(("kc", 64 * h, 64 * h + 64), [[2 * (owners[2 * h + 1] - owners[2 * h]), 2], [1, 2], [0, 16]], 2 * owners[2 * h], 0)

    QV = ("qp", 0, 128)

    def setup():
        ts(OH, CF(58, 60), 0.0, A.is_equal)
        yield
        ts(("wp", 0, 136), ("xi", 0, 136), CF(40), A.is_equal, CF(41), A.mult)
        yield
        ts(("pl", 0, 4), YI(40, 44), CF(6), A.add)
        yield
        for h in range(2):
            ts(("pl", 4 + 2 * h, 6 + 2 * h), YI(44 + 2 * h, 46 + 2 * h), CF(7 + h), A.add)
            yield
        ts(("bm", 0, 144), ("xi", 0, 144), 16.0, A.is_equal, CF(0), A.mult)
        lin(CF(49), CF(0), 64.0, CF(1))
        yield
        ts(("wi", 0, 128), ("xi", 0, 128), 0.0, A.is_equal)
        yield
        ts(("gm", 0, 32), ("xi", 0, 32), PART, A.add, CF(44), A.is_equal)
        yield
        ts(("bh", 0, 144), ("xi", 0, 144), CF(48), A.is_equal, CF(49), A.mult)
        yield
        if OPT["pid"]:
            ts(("we", 0, 128), ("xi", 0, 128), 0.0, A.is_equal)
            yield

    def setup2():
        for d in range(1, 6):
            ts(("sb", 128 * d - 128, 128 * d), ("qo", 0, 128), float(S[d] - S[1] + PAD), A.is_ge, 2.0 ** -d, A.mult)
            yield
        mm(PS(7, 0, 128), [(("wi", 0, 128), ("sb", 128 * d, 128 * d + 128)) for d in range(5)])
        tt(("qi", 0, 128), PS(6, 0, 128), QV, A.min)
        yield
        ts(("m2", 0, 128), PS(7, 0, 128), -1.0, A.add)
        yield
        cp(("qo", 128, 256), ("qi", 0, 128))
        yield

    early, more = setup(), setup2()

    def some(k, gen=early):
        for _ in range(k):
            if next(gen, "end") != "end":
                yield

    def asked(h):
        gather("v", sub(QV, 64 * h, 64 * h + 64), ("qv", 64 * h, 64 * h + 64), ("pl", 4 * h, 4 * h + 4))
        ts(QO(h), sub(QV, 64 * h, 64 * h + 64), float(S[1] - PAD), A.subtract)

    for i in range(2):
        mm(PS(6 + i, 256, 384), [(("wx", 256 * i + 128 * side, 256 * i + 128 * side + 128), ("lh", 128 * side, 128 * side + 128))
                                 for side in (0, 1)])
        cp(("lx", 128 * i, 128 * i + 128), PS(6 + i, 256, 384))
    ts(("off", 120, 240), ("ri", 128, 248), float(S[1] - PAD), A.subtract)
    ts(("off", 0, 120), ("li", 128, 248), float(S[1] - PAD), A.subtract)
    for s in range(16):
        mm(PS(s // 2, 128 * (s % 2), 128 * (s % 2) + 128),
           [(("ws", 128 * s, 128 * s + 128), ("lx", 128 * (s // 8), 128 * (s // 8) + 128))])
    for s in range(16):
        o, src = ("big", PAD + s, PAD + 2048, 16), PS(s // 2, 128 * (s % 2), 128 * (s % 2) + 128)
        if OPT["ev"][s // 2] == "a":
            act(o, src, OFS)
        else:
            ts(o, src, OFS, A.add)
            if s % 2:
                run(some(2))

    for d, cuts, k in OPT["cuts"]:
        win = ("big", 0, G(d, 0, 0)[1])
        for a, m in [(x, y - x) for x, y in zip(cuts, cuts[1:])]:
            t, col = ("xa", a, a + m), CF(15 + d)
            if a or not OPT["own"]:
                op("a", lambda: g.scalar.activation(ap(t), ap(win).indirect(ap(OFF(d, 1, a, a + m))), F.Identity, bias=ap(col)),
                   [win, OFF(d, 1, a, a + m), col], [t])
            else:
                op("v", lambda: V.tensor_scalar(ap(t), ap(win).indirect(ap(OFF(d, 1, a, a + m))), ap(col), None, A.add),
                   [win, OFF(d, 1, a, a + m), col], [t])
            if not a:
                run(some(k))
            op("v", lambda: V.tensor_tensor(ap(G(d, a, a + m)), ap(win).indirect(ap(OFF(d, 0, a, a + m))), ap(t), A.max),
               [win, OFF(d, 0, a, a + m), t], [G(d, a, a + m)])
    win = ("big", 0, G(5, 0, 0)[1])
    for side in (0, 1):
        gather("v", ("pi", side, 256, 2), win, OFF(5, side, 0, 128))
    gather("a", G(5, 0, 128), win, OFF(5, 0, 0, 128))
    run(early)
    W1, W2, WW = OPT["wide"]

    LF = ("lf", 0, 4096)

    def leaves(e, a, b):
        if b > a:
            gather(e, ("c1", a, b), LF, ("pi", a // 16, b // 16))

    def words(c):
        for side in (0, 1):
            mm(PS(c // 2, 256 * side + 128 * (c % 2), 256 * side + 128 * (c % 2) + 128) if W1 else PS(c, 128 * side, 128 * side + 128),
               [(("wp", 3 - k, 131 - k), ("c1", 1024 * c + 256 * k + side, 1024 * c + 256 * k + 256, 2)) for k in range(4)])

    def empty_bits(a, b):
        ts(b, a, 1, A.logical_shift_right, M21, A.bitwise_and)
        yield
        ts(b, b, -1.0, A.mult, float(32 * ONES), A.add)
        yield
        ts(b, b, 5, A.logical_shift_right, ONES, A.bitwise_and)
        yield

    def fitch(a, b, outs, spare=None, src=None):
        yield from empty_bits(a, b)
        t = spare or b
        ts(t, b, 21.0, A.mult)
        yield
        tt(b, t, src or a, A.add)
        yield
        for s, out in enumerate(outs):
            ts(out, sub(b, s, b[2] - b[1], len(outs)), 1, A.logical_shift_right, M21, A.bitwise_and)
            yield

    def up(d, lo, hi, i):
        a, b = ("ta", 512 * i, 512 * i + hi - lo), ("tb", 512 * i, 512 * i + hi - lo)
        tt(a, H(d - 1, 0, lo, hi), H(d - 1, 1, lo, hi), A.add)
        yield
        outs = [H(d, s, lo // 2, hi // 2) for s in (0, 1)] if d < 5 else [H(d, 0, lo, hi)]
        yield from fitch(a, b, outs, PS(4 + i, 0, hi - lo) if hi - lo > 32 else None)

    def level1(c, i, m):
        w = ("tb", 512 * i, 512 * i + 2 * m)
        cp(w, PS(c, 0, 2 * m))
        yield
        for s in (0, 1):
            ts(H(0, s, m * c, m * c + m), sub(w, m * s, m * s + m), M21, A.bitwise_and)
            yield
        yield from up(1, m * c, m * c + m, i)

    def table(cls, levels, halves=(0, 1)):
        srcs = [(("uf", "us", "af")[cls], B[d] + h * (512 >> d), B[d] + (h + 1) * (512 >> d)) for d in levels for h in halves]
        outs = [("big", 4 * x[1], 4 * x[2], 1, cls) for x in srcs]
        sem = "t%d%d%d" % (cls, levels[0], halves[0])
        order("s", srcs, outs)
        for src, out in zip(srcs, outs):
            g.sync.dma_start(T.big[cls:128:4, out[1]:out[2]], ap(src)).then_inc(T.sem[sem], 16)
        note((sem, 16 * len(srcs)), srcs, outs)

    def words_out(cls, a, b):
        for s in (0, 1):
            widen((("uf", "us")[cls], a + s, b, 2), ("u", 1024 * (s ^ cls) + a // 2, 1024 * (s ^ cls) + b // 2))

    LC = (0,) if OPT["sg"] else (0, 1)

    def half_out(d, h):
        for cls in (0, 1) if d else LC:
            words_out(cls, B[d] + h * (512 >> d), B[d] + (h + 1) * (512 >> d))
            if d and not h:
                table(cls, (d,), (h,))
        yield

    def to_list(out, src, wt="bm"):
        w = src[2] - src[1]
        mm(out, [((wt, 16 - s, 144 - s), sub(src, s, w, 16)) for s in range(16)])

    POS = ("pos", 0, 4096)

    def spread(e, a, b):
        scatter(e, POS, ("pi", a // 16, b // 16), ("pay", a, b))

    def leftmost(h):
        x = ("xa", 1024 * h, 1024 * h + 1024)
        gather("a", x, ("big", 0, 4096), QO(h))
        to_list(PS(6, 64 * h, 64 * h + 64), x)

    for c in range(4):
        m = 1024 * c + OPT["lv"][c]
        leaves("v", 1024 * c, m)
        leaves("a", m, 1024 * c + 1024)
        words(c)
        if c == 0:
            asked(1)
    leftmost(1)
    spread("a", 0, OPT["llc"])

    def clades():
        asked(0)
        leftmost(0)
        spread("a", OPT["llc"], 4096)
        yield

    def first_half():
        yield from late(3, half_out(0, 0))
        yield from late(6, half_out(1, 0))

    run(level1(0, 0, 256), late(OPT["l1"], level1(1, 1, 256)), late(OPT["a0"], clades()), first_half(),
        late(OPT["l1"] + 3, half_out(0, 1)))
    run(half_out(1, 1))
    for h in range(2):
        for cls in LC:
            table(cls, (0,), (h,))
    for cls in (0, 1):
        table(cls, (1,), (1,))
    if W2:
        run(up(2, 0, 256, 0), late(1, some(5, more)))
        run(up(3, 0, 128, 0))
    else:
        run(up(2, 0, 128, 0), late(2, up(2, 128, 256, 1)))
        run(up(3, 0, 128, 0), late(1, some(5, more)))
    for cls in (0, 1):
        words_out(cls, B[2], B[4])
        table(cls, (2, 3))
    run(up(4, 0, 64, 0), late(2, some(3, more)))
    for cls in (0, 1):
        words_out(cls, B[4], B[5])
        table(cls, (4,))

    def sums(d, out, par, lo, hi):
        for s in (0, 1):
            tt(sub(out, 2 * lo + s, 2 * hi, 2), H(d, 1 - s, lo, hi), sub(par, lo, hi), A.add)
            yield

    def down3():
        for s in (0, 1):
            cp(("o", 128 + s, 192, 2), H(4, 1 - s, 0, 32))
            yield
        yield from sums(3, ("ai", 256, 384), ("o", 128, 192), 0, 64)
        yield from fitch(("ai", 256, 384), ("tb", 512, 640), [("o", 0, 128)], PS(5, 0, 128))

    def down2(i, m):
        yield from sums(2, ("ai", 0, 256), ("o", 0, 128), m // 2 * i, m // 2 * (i + 1))
        yield from fitch(("ai", m * i, m * i + m), ("tb", 512 * i, 512 * i + m), [("o", 192 + m * i, 192 + m * i + m)],
                         PS(4 + i, 0, m))
        for s in (0, 1):
            cp(("af", B[1] + 2 * m * i + s, B[1] + 2 * m * (i + 1), 2), ("o", 192 + m * i, 192 + m * i + m))
            if s:
                table(2, (1,), (i,) if m == 128 else (0, 1))
            yield


    def lookup(e, h, a, b):
        gather(e, ("xh", 1024 * h + a, 1024 * h + b), POS, QO(2 + h, a // 16, b // 16))

    def listed(h, a=0, b=64):
        to_list(PS(7 - h - 3 * (a > 0), a, b), ("xh", 1024 * h + 16 * a, 1024 * h + 16 * b), "bh")

    def index(h, a=0, b=64):
        t = QI(3 + h, a, b)
        tt(t, PS(7 - h - 3 * (a > 0), a, b), ("m2", 64 * h + a, 64 * h + b), A.mult)
        if h:
            ts(QO(6, a, b), t, 0.5, A.mult, 4095.75, A.add)
        ts(QO(4 + h, a, b), t, 8192.0, A.add)

    def sibling():
        ts(QI(5), QO(6), 4.0, A.mult, -8191.0, A.add)
        tt(QI(5), QI(5), QI(4), A.subtract)
        tt(QI(5), QI(5), QI(7), A.max)
        cp(QO(7), QI(5))

    TAB = ("big", 0, 8192)

    def moved(q, sem, cls, out, x):
        order(q, [x], [out])
        Q[q].dma_start(ap(out), T.xv[cls:128:4, x[1]:x[2]]).then_inc(T.sem[sem], 16)
        note((sem, 16), [x], [out])

    def operand(e, i, h):
        x = ("xv", 1024 * (i + 1) + 512 * h, 1024 * (i + 1) + 512 * h + 512)
        if (i, h) in OPT["pe"]:
            for k in range(4):
                y = sub(x, 128 * k, 128 * k + 128)
                gather(e, y, ("big", 4096, 8192), QO(6, 32 * h + 8 * k, 32 * h + 8 * k + 8))
                op("p", lambda: g.tensor.matmul(ap(PS(1 + h, 0, 128)), T.we[:, 131 - k:259 - k], ap(y), k == 0, k == 3),
                   [y, ("we", 128, 264)], [PS(1 + h, 0, 128)])
            return
        if OPT["sg"] and i:
            gather(e, x, TAB, QO(3 + 2 * i, 32 * h, 32 * h + 32))
            c = 256 * (4 - i) + 128 * h
            moved("s", "d%d" % (8 - 2 * i + h), 0, ("so", c, c + 128), x)
            return
        gather(e, x, TAB if i else ("big", 4096, 8192), QO(6 - i, 32 * h, 32 * h + 32))
        for j, cls in enumerate((1, 0) if i else (2, 1)):
            c = 256 * (2 * i + j) + 128 * h
            moved("s", "d%d" % (4 * i + 2 * j + h), cls, ("so", c, c + 128), x)

    def answer(e, h):
        x, out = ("xv", 512 * h, 512 * h + 512), ("land", 128 * h, 128 * h + 128)
        if h == 0 and OPT["pc"]:
            for k in range(4):
                y = sub(x, 128 * k, 128 * k + 128)
                gather(e, y, TAB, QO(4, 8 * k, 8 * k + 8))
                op("p", lambda: g.tensor.matmul(ap(PS(0, 0, 128)), T.we[:, 267 - k:395 - k], ap(y), k == 0, k == 3),
                   [y, ("we", 264, 400)], [PS(0, 0, 128)])
            return
        gather(e, x, TAB, QO(4, 32 * h, 32 * h + 32))
        moved("s", "dc%d" % h, 0, out, x)
        reply(h)

    def out_of_psum(e):
        (act if e == "a" else cp)(("land", 0, 128), PS(0, 0, 128))
        reply(0)

    def reply(h):
        send([d for d in dests if (hops[d] == d) == bool(h)], lambda d: ("land", 64 * ring.index(d), 64 * ring.index(d) + 64),
             lambda d: ("land", lands_at(core, d, T, topo), lands_at(core, d, T, topo) + 64), T.sem.rp)

    note(("rp", come[True]), [], [("land", 256, 320)])
    note(("rp2", come[False]), [], [("land", 320, 448)])

    run(up(5, 0, 32, 0), down3(), late(2, more))
    widen(("uf", B[5], B[6]), H(5, 0, 0, 32))
    table(0, (5,))
    for s in (0, 1):
        widen(("af", B[2] + s, B[4], 2), ("o", 0, 192))
    table(2, (2, 3))
    steps = {"L": lookup, "T": listed, "I": index, "O": operand, "A": answer, "R": out_of_psum, "S": sibling}

    def take(sts):
        for st in sts:
            steps[st[0]](*st[1:])
        yield

    if W2:
        run(down2(0, 256), late(OPT["ic"], take(OPT["mid"])))
    else:
        run(down2(0, 128), late(2, down2(1, 128)), late(OPT["ic"], take(OPT["mid"])))
    run(take(OPT["tail"]))
    lin(("kc", 0, 128), ("kc", 0, 128), 0.125, 0.0)

    def low(e, fn, reads, writes):
        op(e, lambda: fn(*[T[r[0]][0:64, r[1]:r[2]] for r in writes + reads]), reads, writes)

    def walk(h, m):
        lo, hi = m * h, m * h + m
        a, b, x = ("ta", lo, hi), ("tb", lo, hi), ("o", lo, hi)
        spare = PS(1 + h, 0, m)
        for i in (1, 2, 3):
            y = ("so", 256 * i + lo, 256 * i + hi)
            if i == 1 and OPT["pid"]:
                for j in (2, 3):
                    mm(PS(3 + h, m * j - 2 * m, m * j - m), [(("we", 0, 128), ("so", 256 * j + lo, 256 * j + hi))])
            if i > 1 and OPT["pid"]:
                y = PS(3 + h, m * i - 2 * m, m * i - m)
            tt(a, x if i > 1 else ("so", lo, hi), y, A.add)
            yield
            yield from fitch(a, b, [x], spare)
        tt(a, x, ("land", 192 + lo, 192 + hi), A.add)
        yield
        yield from empty_bits(a, b)
        cp(("nzf", lo, hi), b)
        for j in range(lo // 64, hi // 64):
            o, y = PS(7, 32 * j, 32 * j + 32), ("nzf", 64 * j, 64 * j + 64)
            op("p", lambda: g.tensor.matmul(T[o[0]][0:64, o[1]:o[2]], ap(y), T.gm[:, 0:32], True, True), [y, ("gm", 0, 32)], [o])
        yield

    if WW:
        run(walk(0, 256))
    else:
        run(walk(0, 128), late(OPT["lag"], walk(1, 128)))
    k, f = ("ki", 0, 128), ("kf", 0, 128)
    low("v", lambda o, y: V.tensor_scalar(o, y, ONES / 262144.0, None, A.mult), [PS(7, 0, 128)], [k])
    low("v", lambda o, y: V.tensor_scalar(o, y, 63, None, A.bitwise_and), [k], [k])
    low("v", lambda o, y, z: V.tensor_tensor(o, y, z, A.add), [k, ("kc", 0, 128)], [f])
    low("v", lambda o, y, z: V.tensor_tensor(o, y, z, A.min), [sub(f, 0, 64), sub(f, 64, 128)], [("kf", 128, 192)])
    low("v", lambda o, y, z: V.tensor_tensor(o, y, z, A.min), [("kf", 128, 160), ("kf", 160, 192)], [("kf", 192, 224)])
    low("v", lambda o, y, z: V.tensor_tensor(o, y, z, A.min), [("kf", 192, 208), ("kf", 208, 224)], [("kb", 0, 16)])
    for h in range(2):
        op("p", lambda: g.tensor.matmul(T.ps5[0:8, 64 * h:64 * h + 64], T.kb[0:64, 8 * h:8 * h + 8], T.wi[0:64, 0:64], True, True),
           [("kb", 0, 16), ("wi", 0, 64)], [PS(5, 64 * h, 64 * h + 64)])
    op("v", lambda: V.tensor_scalar(T.ei[0:8, :], T.ps5[0:8, 0:128], -0.4375, None, A.add), [PS(5, 0, 128)], [("ei", 0, 128)])
    op("v", lambda: V.tensor_copy(T.ef[0:8, 0:128], T.ei[0:8, :]), [("ei", 0, 128)], [("ef", 0, 128)])
    order("s", [("ef", 0, 128)], [])
    g.sync.dma_start(T.cost[:], T.ef[0:8, 0:128]).then_inc(T.sem.do1, 16)
    op("v", lambda: V.tensor_tensor(T.ef[0:8, 256:384], T.ps5[0:8, 0:128], T.ei[0:8, :], A.subtract),
       [PS(5, 0, 128), ("ei", 0, 128)], [("ef", 256, 384)])
    op("v", lambda: V.tensor_scalar(T.ef[0:8, 128:256], T.ef[0:8, 256:384], 8.0, None, A.mult),
       [("ef", 256, 384)], [("ef", 128, 256)])
    order("a", [("ef", 128, 256)], [])
    g.scalar.dma_start(T.first[:], T.ef[0:8, 128:256]).then_inc(T.sem.do2, 16)

    for e in cnt:
        wait("g", (e, cnt[e]))
    wait("g", ("snt", sent))
    wait("g", ("do1", 16))
    wait("g", ("do2", 16))
